import numpy as np
import ml_dtypes


def mxq(x, axis, fmt="e4m3"):
    dtype, down = {"e4m3": (ml_dtypes.float8_e4m3fn, 7), "e5m2": (ml_dtypes.float8_e5m2, 14)}[fmt]
    v = np.moveaxis(np.asarray(x, np.float32).astype(ml_dtypes.bfloat16).astype(np.float64), axis, -1)
    blocks = v.reshape(v.shape[:-1] + (-1, 32))
    amax = np.abs(blocks).max(-1, keepdims=True)
    byte = np.maximum(np.where(amax > 0, np.frexp(amax)[1] - 1 + 127, 0) - down, 1)
    scale = np.exp2(byte - 127.0)
    codes = (blocks / scale).astype(np.float32).astype(dtype).astype(np.float64)
    return np.moveaxis((codes * scale).reshape(v.shape), -1, axis)


WIDE = False


def mx_kscale(k):
    if not WIDE:
        return np.ones(k)
    levels = np.array([10, -10, 5, -5, 0])
    if k % 512:
        return np.exp2(np.random.permutation(np.resize(levels, k // 32))).repeat(32)
    a = np.empty((k // 512, 16))
    for p in range(k // 512):
        a[p, :8] = np.random.permutation(np.resize(levels, 8))
        for g in range(8):
            far = levels[np.abs(levels - a[p, g]) >= 10]
            a[p, g + 8] = far[np.random.randint(len(far))]
    return np.exp2(a.ravel()).repeat(32)


BF16 = ml_dtypes.bfloat16


def bf(x):
    return np.asarray(x, np.float32).astype(BF16)


def f64(x):
    return np.asarray(x).astype(np.float64)


N, D, M = 2048, 1024, 1024


def draw0():
    s = mx_kscale(D)
    u = mx_kscale(N)
    return {
        "x": bf(np.random.standard_normal((N, D)) * s),
        "w": bf(np.random.standard_normal((D, M)) / np.sqrt(D) / s[:, None]),
        "c": bf(0.2 * np.random.standard_normal(M)),
        "k": bf(np.random.standard_normal(M)),
        "a": bf((1.0 + 0.3 * np.random.standard_normal(N)) * u),
        "b": bf((1.0 + 0.3 * np.random.standard_normal(N)) / u),
    }


def core(x, w, c, k, a, b):
    root_n = np.sqrt(x.shape[0])
    y = (mxq(f64(x), 1, "e4m3") @ mxq(f64(w), 0, "e4m3")) + f64(c)[None, :]
    f = (y + f64(k)[None, :] * np.tanh(y)) * f64(a)[:, None]
    h = y * f64(b)[:, None]
    m = (mxq(f, 0, "e4m3").T @ mxq(h, 0, "e4m3")) / root_n
    return -m + root_n * np.eye(w.shape[1])


def e4m3fn_bytes(y):
    return np.clip(np.asarray(y, np.float64), -448.0, 448.0).astype(np.float32).astype(ml_dtypes.float8_e4m3fn).view(np.uint8)


def e4m3fn_values(b):
    return np.asarray(b, np.uint8).view(ml_dtypes.float8_e4m3fn).astype(np.float64)


def setup_inputs():
    d = draw0()
    x0 = np.asarray(d['x']).astype(np.float64)
    s = (np.max(np.abs(x0), axis=(0,), keepdims=True) / 448.0).astype(np.float32)
    out = {}
    for k, v in d.items():
        if k == 'x':
            out['x_bytes'] = e4m3fn_bytes(x0 / s.astype(np.float64))
            out['x_scale'] = s
        else:
            out[k] = v
    return out


def reference(x_bytes, x_scale, w, c, k, a, b):
    return core(e4m3fn_values(x_bytes) * x_scale.astype(np.float64), w, c, k, a, b)

@@ -1,0 +1,371 @@
+import math
+from contextlib import ExitStack
+
+import concourse.mybir as mybir
+from concourse.masks import make_identity
+
+N, D, M = 2048, 1024, 1024
+FLOPS = 2 * N * D * M + 2 * N * M * M
+
+F32 = mybir.dt.float32
+BF16 = mybir.dt.bfloat16
+U32 = mybir.dt.uint32
+U8 = mybir.dt.uint8
+FP8 = mybir.dt.float8_e4m3fn
+FP8X4 = mybir.dt.float8_e4m3fn_x4
+ALU = mybir.AluOpType
+ACT = mybir.ActivationFunctionType
+
+P = 128
+PASS = 512
+GROUPS = N // PASS
+KP = D // PASS
+CHUNKS = M // P
+ROOT_N = math.sqrt(N)
+
+STEPS = [(0, 1), (2, 3), (4,), (5,), (6,), (7,)]
+JOBS = [
+    [[(0, 2, 0, 256)]],
+    [[(2, 1, 0, 512)], [(3, 1, 0, 512)], [(0, 2, 256, 256)]],
+    [[(4, 1, 0, 512)], [(0, 4, 512, 128)]],
+    [[(5, 1, 0, 512)], [(0, 4, 640, 128)], [(4, 2, 512, 256)]],
+    [[(6, 1, 0, 512)], [(0, 4, 768, 128)], [(6, 1, 512, 256), (4, 2, 768, 128)]],
+    [[(7, 1, 512, 512)], [(6, 1, 768, 256), (4, 2, 896, 128)], [(7, 1, 0, 512)], [(0, 4, 896, 128)]],
+]
+
+
+def tile_extendedinfomaxicarelativegrad_kernel(tc, x_bytes, x_scale, w, c, k, a, b, out):
+    nc = tc.nc
+    with ExitStack() as ctx:
+        keep = ctx.enter_context(tc.tile_pool(name="keep", bufs=1))
+        work = ctx.enter_context(tc.tile_pool(name="work", bufs=3))
+        psum = ctx.enter_context(tc.psum_pool(name="psum", bufs=1))
+        ctx.enter_context(tc.manual_schedule())
+
+        def bank(index, dtype=F32):
+            width = 512 if dtype == F32 else 1024
+            return psum.tile([P, width], dtype, name="bank%d" % index, tag="bank%d" % index)
+
+        ident = keep.tile([P, P], F32, name="ident", align_bytes=64)
+        make_identity(nc, ident[:])
+        ck_rows = keep.tile([P, P], BF16, name="ck_rows", align_bytes=64)
+        nc.gpsimd.memset(ck_rows[:], 0.0)
+        ident_bf = keep.tile([P, P], BF16, name="ident_bf", align_bytes=64)
+        make_identity(nc, ident_bf[:])
+        root_ident = keep.tile([P, P], F32, name="root_ident", align_bytes=64)
+        nc.gpsimd.tensor_scalar(out=root_ident[:], in0=ident[:], scalar1=ROOT_N, scalar2=0.0, op0=ALU.mult, op1=ALU.add)
+
+        scale_cols = keep.tile([P, KP, 4], F32, name="scale_cols", align_bytes=64)
+        nc.sync.dma_start(out=scale_cols[:], in_=x_scale.rearrange("o (g p t) -> p (o g) t", p=P, t=4))
+
+        x_view = x_bytes.rearrange("(g q j) d -> g q j d", q=P, j=4)
+        w_view = w.rearrange("(g p t) m -> g p t m", p=P, t=4)
+        xb = {}
+        w_raw = {}
+
+        def load_x(g):
+            for u in range(2):
+                xb[g, u] = keep.tile([P, 2, D], U8, name="xbytes%d%d" % (g, u), align_bytes=256)
+                nc.sync.dma_start(out=xb[g, u][:], in_=x_view[g, :, 2 * u : 2 * u + 2, :])
+
+        def load_w(q):
+            for kp in range(KP):
+                w_raw[q, kp] = keep.tile([P, 4, 256], BF16, name="wraw%d%d" % (q, kp), align_bytes=256)
+                nc.sync.dma_start(out=w_raw[q, kp][:], in_=w_view[kp, :, :, 256 * q : 256 * (q + 1)])
+
+        load_x(0)
+        load_w(0)
+        load_x(1)
+        nc.sync.dma_start(out=ck_rows[0:CHUNKS, :], in_=c.rearrange("(i p) -> i p", p=P))
+        nc.sync.dma_start(out=ck_rows[CHUNKS : 2 * CHUNKS, :], in_=k.rearrange("(i p) -> i p", p=P))
+        ab_cols = []
+        for name, vec in (("a_cols", a), ("b_cols", b)):
+            cols = keep.tile([P, 16], BF16, name=name, align_bytes=64)
+            nc.sync.dma_start(out=cols[:], in_=vec.rearrange("(n j) -> n j", j=16))
+            ab_cols.append(cols)
+        load_x(2)
+        load_x(3)
+        load_w(1)
+        load_w(2)
+        load_w(3)
+
+        scale_bank = []
+        for kp in range(KP):
+            sb = bank(5 + kp)
+            for t in range(4):
+                nc.tensor.transpose(sb[:, t:512:4], scale_cols[:, kp, t : t + 1].to_broadcast([P, P]), ident[:])
+            scale_bank.append(sb)
+
+        x_units = [(g, kp, u) for g in range(GROUPS) for kp in range(KP) for u in range(2)]
+        x_grouped = {}
+        xq = {}
+        xs = {}
+
+        def x_unit(h):
+            g, kp, u = x_units[h]
+            scaled = work.tile([P, 2, PASS], BF16, name="x_scaled", bufs=4, align_bytes=256)
+            for e in range(2):
+                nc.vector.tensor_tensor(
+                    out=scaled[:, e, :],
+                    in0=xb[g, u][:, e, kp * PASS : (kp + 1) * PASS].bitcast(FP8),
+                    in1=scale_bank[kp][:],
+                    op=ALU.mult,
+                )
+            words = scaled[:].rearrange("p e d -> p (e d)").bitcast(F32)
+            tb = bank((3, 4, 7)[h % 3])
+            for e in range(2):
+                for v in range(2):
+                    s = 2 * e + v
+                    nc.tensor.transpose(tb[:, s * P : (s + 1) * P], words[:, 256 * e + v : 256 * (e + 1) : 2], ident[:])
+            if u == 0:
+                x_grouped[g, kp] = work.tile([P, 4 * PASS], BF16, name="x_grouped", bufs=3, align_bytes=256)
+            dst = x_grouped[g, kp][:].bitcast(F32)[:, 512 * u : 512 * (u + 1)]
+            nc.scalar.copy(out=dst.rearrange("p (q s) -> p q s", s=4), in_=tb[:].rearrange("p (s q) -> p q s", s=4))
+
+        def x_quant(j):
+            g, kp = divmod(j, KP)
+            xq[g, kp] = keep.tile([P, PASS], U32, name="xq%d" % j, align_bytes=256)
+            xs[g, kp] = keep.tile([P, PASS], U8, name="xs%d" % j, align_bytes=256)
+            nc.vector.quantize_mx(out=xq[g, kp][:].bitcast(FP8X4), scales=xs[g, kp][:], in_=x_grouped[g, kp][:])
+
+        w_grouped = {}
+        wq = {}
+        ws = {}
+
+        def w_interleave(q, kp):
+            if kp == 0:
+                w_grouped[q] = work.tile([P, KP * 1024], BF16, name="w_grouped", bufs=2, align_bytes=256)
+            dst = w_grouped[q][:, 1024 * kp : 1024 * (kp + 1)]
+            nc.scalar.copy(out=dst.rearrange("p (m t) -> p m t", t=4), in_=w_raw[q, kp][:].rearrange("p t m -> p m t"))
+
+        def w_quant(q):
+            wq[q] = keep.tile([P, KP * 256], U32, name="wq%d" % q, align_bytes=256)
+            ws[q] = keep.tile([P, KP * 256], U8, name="ws%d" % q, align_bytes=256)
+            nc.vector.quantize_mx(out=wq[q][:].bitcast(FP8X4), scales=ws[q][:], in_=w_grouped[q][:])
+
+        ck = keep.tile([P, 2 * CHUNKS], F32, name="ck", align_bytes=64)
+
+        def make_ck():
+            cb = bank(0, BF16)
+            nc.tensor.transpose(cb[:, 0:P], ck_rows[:], ident_bf[:])
+            nc.scalar.copy(out=ck[:], in_=cb[:, 0 : 2 * CHUNKS])
+
+        ab_rows = [keep.tile([P, N], BF16, name="a_rows", align_bytes=256), keep.tile([P, N], BF16, name="b_rows", align_bytes=256)]
+
+        def make_ab(j):
+            which, u = divmod(j, 2)
+            sb = bank((1, 2, 0, 1)[j])
+            words = ab_cols[which][:].bitcast(F32)
+            for r in range(4):
+                col = 2 * r + u
+                nc.tensor.transpose(sb[:, r * P : (r + 1) * P], words[:, col : col + 1].to_broadcast([P, P]), ident[:])
+            dst = ab_rows[which][:].bitcast(F32).rearrange("p (g u s r) -> p g u s r", g=GROUPS, u=2, r=4)[:, :, u, :, :]
+            nc.scalar.copy(out=dst, in_=sb[:].rearrange("p (r g s) -> p g s r", r=4, g=GROUPS))
+
+        units = [(s, g, i) for s, chunks in enumerate(STEPS) for g in range(GROUPS) for i in chunks]
+        n_units = len(units)
+        y_bank = {}
+        th = {}
+        f_t = {}
+        h_t = {}
+        fh_grouped = {}
+        fq = [keep.tile([P, M], U32, name="fq%d" % g, align_bytes=256) for g in range(GROUPS)]
+        fs = [keep.tile([P, M], U8, name="fs%d" % g, align_bytes=256) for g in range(GROUPS)]
+        hq = [keep.tile([P, M], U32, name="hq%d" % g, align_bytes=256) for g in range(GROUPS)]
+        hs = [keep.tile([P, M], U8, name="hs%d" % g, align_bytes=256) for g in range(GROUPS)]
+
+        def y_matmul(n):
+            s, g, i = units[n]
+            q, half = divmod(i, 2)
+            y_bank[n] = bank(n % 3)
+            for kp in range(KP):
+                cols = slice(256 * kp + P * half, 256 * kp + P * (half + 1))
+                nc.tensor.matmul_mx(
+                    out=y_bank[n][:],
+                    lhsT=wq[q][:, cols].bitcast(FP8X4),
+                    lhsT_scale=ws[q][:, cols],
+                    rhs=xq[g, kp][:].bitcast(FP8X4),
+                    rhs_scale=xs[g, kp][:],
+                    start=(kp == 0),
+                    stop=(kp == KP - 1),
+                )
+
+        def y_tanh(n):
+            s, g, i = units[n]
+            th[n] = work.tile([P, PASS], F32, name="th", bufs=4, align_bytes=256)
+            nc.scalar.activation(out=th[n][:], in_=y_bank[n][:], func=ACT.Tanh, bias=ck[:, i : i + 1], scale=1.0)
+
+        def elementwise(n):
+            s, g, i = units[n]
+            tokens = slice(PASS * g, PASS * (g + 1))
+            part = work.tile([P, PASS], F32, name="part", bufs=2, align_bytes=256)
+            nc.vector.scalar_tensor_tensor(
+                out=part[:], in0=th[n][:], scalar=ck[:, CHUNKS + i : CHUNKS + i + 1], in1=y_bank[n][:], op0=ALU.mult, op1=ALU.add
+            )
+            h_t[n] = work.tile([P, PASS], BF16, name="h_t", bufs=3, align_bytes=256)
+            nc.vector.scalar_tensor_tensor(
+                out=h_t[n][:], in0=y_bank[n][:], scalar=ck[:, i : i + 1], in1=ab_rows[1][:, tokens], op0=ALU.add, op1=ALU.mult
+            )
+            f_t[n] = work.tile([P, PASS], BF16, name="f_t", bufs=3, align_bytes=256)
+            nc.vector.scalar_tensor_tensor(
+                out=f_t[n][:], in0=part[:], scalar=ck[:, i : i + 1], in1=ab_rows[0][:, tokens], op0=ALU.add, op1=ALU.mult
+            )
+
+        turned = {}
+
+        def turn(n):
+            turned[n] = bank(3 + n % 2)
+            for j, src in enumerate((h_t[n], f_t[n])):
+                words = src[:].bitcast(F32)
+                for u in range(2):
+                    s = 2 * j + u
+                    nc.tensor.transpose(turned[n][:, s * P : (s + 1) * P], words[:, u * P : (u + 1) * P], ident[:])
+
+        def regroup(n):
+            s, g, i = units[n]
+            width = len(STEPS[s])
+            place = STEPS[s].index(i)
+            if place == 0:
+                fh_grouped[s, g] = work.tile([P, 2 * width * PASS], BF16, name="fh_grouped", bufs=3, align_bytes=256)
+            words = fh_grouped[s, g][:].bitcast(F32).rearrange("p (j i m u) -> p j i m u", j=2, i=width, u=2)
+            nc.scalar.copy(out=words[:, :, place, :, :], in_=turned[n][:].rearrange("p (j u m) -> p j m u", j=2, u=2))
+
+        def fh_quant(n):
+            s, g, i = units[n]
+            if i != STEPS[s][-1]:
+                return
+            width = len(STEPS[s])
+            cols = slice(P * STEPS[s][0], P * (i + 1))
+            for j, (codes, scales) in enumerate(((hq, hs), (fq, fs))):
+                nc.vector.quantize_mx(
+                    out=codes[g][:, cols].bitcast(FP8X4),
+                    scales=scales[g][:, cols],
+                    in_=fh_grouped[s, g][:, j * width * PASS : (j + 1) * width * PASS],
+                )
+
+        def sums_of(job):
+            sums = []
+            place = 0
+            for row0, rows, col0, width in job:
+                for r in range(rows):
+                    sums.append((row0 + r, col0, width, place))
+                    place = place + width
+            return sums
+
+        def m_pass(acc, one_sum, g, start, stop):
+            row, col0, width, place = one_sum
+            rows = slice(P * row, P * (row + 1))
+            cols = slice(col0, col0 + width)
+            nc.tensor.matmul_mx(
+                out=acc[:, place : place + width],
+                lhsT=fq[g][:, rows].bitcast(FP8X4),
+                lhsT_scale=fs[g][:, rows],
+                rhs=hq[g][:, cols].bitcast(FP8X4),
+                rhs_scale=hs[g][:, cols],
+                start=start,
+                stop=stop,
+            )
+
+        def finish(job, acc, on_vector):
+            result = work.tile([P, 512], F32, name="result", bufs=6, align_bytes=256)
+            if on_vector:
+                nc.vector.tensor_scalar(out=result[:], in0=acc[:], scalar1=-1.0 / ROOT_N, scalar2=None, op0=ALU.mult)
+            else:
+                nc.scalar.activation(out=result[:], in_=acc[:], func=ACT.Copy, scale=-1.0 / ROOT_N)
+            return result
+
+        def diagonal_and_store(job, result):
+            for row, col0, width, place in sums_of(job):
+                if col0 <= P * row < col0 + width:
+                    at = place + P * row - col0
+                    nc.vector.tensor_tensor(out=result[:, at : at + P], in0=result[:, at : at + P], in1=root_ident[:], op=ALU.add)
+            place = 0
+            for row0, rows, col0, width in job:
+                nc.sync.dma_start(
+                    out=out[P * row0 : P * (row0 + rows), col0 : col0 + width].rearrange("(r p) m -> p r m", p=P),
+                    in_=result[:, place : place + rows * width].rearrange("p (r m) -> p r m", r=rows),
+                )
+                place = place + rows * width
+
+        for h in range(len(x_units)):
+            x_unit(h)
+            if h % 2 == 1 and h >= 3:
+                x_quant((h - 3) // 2)
+            if h in (1, 3):
+                w_interleave(0, h // 2)
+            if h == 4:
+                make_ck()
+            if 5 <= h < 9:
+                make_ab(h - 5)
+            if h == 6:
+                w_quant(0)
+            if h in (9, 11):
+                w_interleave(1, (h - 9) // 2)
+            if h in (12, 13):
+                y_matmul(h - 12)
+                y_tanh(h - 12)
+
+        jobs = [(s, job) for s in range(len(STEPS)) for job in JOBS[s]]
+        quantised = [0] * len(STEPS)
+        free_banks = [5, 6, 7]
+        accs = []
+        passes_done = [0] * len(jobs)
+        n_finished = 0
+        pending = []
+
+        def open_jobs_and_pass():
+            while len(accs) < len(jobs) and free_banks and quantised[jobs[len(accs)][0]] > 0:
+                index = free_banks[0]
+                free_banks.remove(index)
+                accs.append((bank(index), index))
+            for j in range(n_finished, len(accs)):
+                s, job = jobs[j]
+                sums = sums_of(job)
+                for g in range(passes_done[j], quantised[s]):
+                    for at, one_sum in enumerate(sums):
+                        m_pass(accs[j][0], one_sum, g, g == 0 and at == 0, g == GROUPS - 1 and at == len(sums) - 1)
+                passes_done[j] = quantised[s]
+
+        for n in range(n_units + 1):
+            if n + 2 < n_units:
+                y_matmul(n + 2)
+            if n >= 1:
+                turn(n - 1)
+            if n + 2 < n_units:
+                y_tanh(n + 2)
+            if n >= 1:
+                regroup(n - 1)
+            open_jobs_and_pass()
+            started = []
+            if passes_done[n_finished] == GROUPS:
+                job = jobs[n_finished][1]
+                started.append((job, finish(job, accs[n_finished][0], False)))
+                free_banks.append(accs[n_finished][1])
+                n_finished = n_finished + 1
+            if n in (4, 6, 12, 14):
+                w_interleave(2 + n // 8, (n % 8 - 4) // 2)
+            if n < n_units:
+                elementwise(n)
+                if n + 3 >= n_units:
+                    free_banks.append(n % 3)
+            if n == 0:
+                x_quant(GROUPS * KP - 1)
+            if n in (1, 9, 17):
+                w_quant(1 + n // 8)
+            for job, result in pending:
+                diagonal_and_store(job, result)
+            pending = started
+            if n >= 1:
+                fh_quant(n - 1)
+                s, g, i = units[n - 1]
+                if i == STEPS[s][-1]:
+                    quantised[s] = g + 1
+        for job, result in pending:
+            diagonal_and_store(job, result)
+        open_jobs_and_pass()
+        last = list(range(n_finished, len(jobs)))
+        for first in range(0, len(last), 2):
+            both = last[first : first + 2]
+            results = [finish(jobs[j][1], accs[j][0], j % 2 == 1) for j in both]
+            for j, result in zip(both, results):
+                diagonal_and_store(jobs[j][1], result)

@@ -23,6 +23,10 @@ KP = D // PASS
 CHUNKS = M // P
 ROOT_N = math.sqrt(N)
 
+SHARED_UNITS = 24
+W_ON_GPSIMD = 6
+H, F = 0, 1
+BOTH = (H, F)
 STEPS = [(0, 1), (2, 3), (4,), (5,), (6,), (7,)]
 JOBS = [
     [[(0, 2, 0, 256)]],
@@ -30,7 +34,7 @@ JOBS = [
     [[(4, 1, 0, 512)], [(0, 4, 512, 128)]],
     [[(5, 1, 0, 512)], [(0, 4, 640, 128)], [(4, 2, 512, 256)]],
     [[(6, 1, 0, 512)], [(0, 4, 768, 128)], [(6, 1, 512, 256), (4, 2, 768, 128)]],
-    [[(7, 1, 512, 512)], [(6, 1, 768, 256), (4, 2, 896, 128)], [(7, 1, 0, 512)], [(0, 4, 896, 128)]],
+    [[(0, 4, 896, 128)], [(6, 1, 768, 256), (4, 2, 896, 128)], [(7, 1, 512, 512)], [(7, 1, 0, 512)]],
 ]
 
 
@@ -83,10 +87,10 @@ def tile_extendedinfomaxicarelativegrad_kernel(tc, x_bytes, x_scale, w, c, k, a,
             cols = keep.tile([P, 16], BF16, name=name, align_bytes=64)
             nc.sync.dma_start(out=cols[:], in_=vec.rearrange("(n j) -> n j", j=16))
             ab_cols.append(cols)
-        load_x(2)
-        load_x(3)
         load_w(1)
+        load_x(2)
         load_w(2)
+        load_x(3)
         load_w(3)
 
         scale_bank = []
@@ -118,7 +122,7 @@ def tile_extendedinfomaxicarelativegrad_kernel(tc, x_bytes, x_scale, w, c, k, a,
                     s = 2 * e + v
                     nc.tensor.transpose(tb[:, s * P : (s + 1) * P], words[:, 256 * e + v : 256 * (e + 1) : 2], ident[:])
             if u == 0:
-                x_grouped[g, kp] = work.tile([P, 4 * PASS], BF16, name="x_grouped", bufs=3, align_bytes=256)
+                x_grouped[g, kp] = work.tile([P, 4 * PASS], BF16, name="x_grouped", bufs=4, align_bytes=256)
             dst = x_grouped[g, kp][:].bitcast(F32)[:, 512 * u : 512 * (u + 1)]
             nc.scalar.copy(out=dst.rearrange("p (q s) -> p q s", s=4), in_=tb[:].rearrange("p (s q) -> p q s", s=4))
 
@@ -128,20 +132,28 @@ def tile_extendedinfomaxicarelativegrad_kernel(tc, x_bytes, x_scale, w, c, k, a,
             xs[g, kp] = keep.tile([P, PASS], U8, name="xs%d" % j, align_bytes=256)
             nc.vector.quantize_mx(out=xq[g, kp][:].bitcast(FP8X4), scales=xs[g, kp][:], in_=x_grouped[g, kp][:])
 
-        w_grouped = {}
         wq = {}
         ws = {}
 
-        def w_interleave(q, kp):
-            if kp == 0:
-                w_grouped[q] = work.tile([P, KP * 1024], BF16, name="w_grouped", bufs=2, align_bytes=256)
-            dst = w_grouped[q][:, 1024 * kp : 1024 * (kp + 1)]
-            nc.scalar.copy(out=dst.rearrange("p (m t) -> p m t", t=4), in_=w_raw[q, kp][:].rearrange("p t m -> p m t"))
+        w_grouped = {}
 
-        def w_quant(q):
-            wq[q] = keep.tile([P, KP * 256], U32, name="wq%d" % q, align_bytes=256)
-            ws[q] = keep.tile([P, KP * 256], U8, name="ws%d" % q, align_bytes=256)
-            nc.vector.quantize_mx(out=wq[q][:].bitcast(FP8X4), scales=ws[q][:], in_=w_grouped[q][:])
+        def w_interleave(j):
+            q, kp = divmod(j, KP)
+            src = w_raw[q, kp][:].rearrange("p t m -> p m t")
+            if j < W_ON_GPSIMD:
+                w_grouped[j] = x_grouped[divmod(j, KP)][:, 0:1024]
+                dst = w_grouped[j].rearrange("p (m t) -> p m t", t=4)
+                nc.gpsimd.tensor_scalar(out=dst, in0=src, scalar1=1.0, scalar2=0.0, op0=ALU.mult, op1=ALU.add)
+            else:
+                own = keep.tile([P, 1024], BF16, name="w_grouped%d" % j, align_bytes=256)
+                w_grouped[j] = own[:]
+                nc.scalar.copy(out=w_grouped[j].rearrange("p (m t) -> p m t", t=4), in_=src)
+
+        def w_quant(j):
+            q, kp = divmod(j, KP)
+            wq[q, kp] = keep.tile([P, 256], U32, name="wq%d" % j, align_bytes=256)
+            ws[q, kp] = keep.tile([P, 256], U8, name="ws%d" % j, align_bytes=256)
+            nc.vector.quantize_mx(out=wq[q, kp][:].bitcast(FP8X4), scales=ws[q, kp][:], in_=w_grouped[j])
 
         ck = keep.tile([P, 2 * CHUNKS], F32, name="ck", align_bytes=64)
 
@@ -166,24 +178,31 @@ def tile_extendedinfomaxicarelativegrad_kernel(tc, x_bytes, x_scale, w, c, k, a,
         n_units = len(units)
         y_bank = {}
         th = {}
-        f_t = {}
-        h_t = {}
+        fh_t = {}
+        quantised = [[0, 0] for s in STEPS]
         fh_grouped = {}
         fq = [keep.tile([P, M], U32, name="fq%d" % g, align_bytes=256) for g in range(GROUPS)]
         fs = [keep.tile([P, M], U8, name="fs%d" % g, align_bytes=256) for g in range(GROUPS)]
         hq = [keep.tile([P, M], U32, name="hq%d" % g, align_bytes=256) for g in range(GROUPS)]
         hs = [keep.tile([P, M], U8, name="hs%d" % g, align_bytes=256) for g in range(GROUPS)]
 
+        fh_codes = (hq, fq)
+        fh_scales = (hs, fs)
+        affine = {}
+
+        def on_gpsimd(n):
+            return n % 2 == 0 and n < SHARED_UNITS
+
         def y_matmul(n):
             s, g, i = units[n]
             q, half = divmod(i, 2)
             y_bank[n] = bank(n % 3)
             for kp in range(KP):
-                cols = slice(256 * kp + P * half, 256 * kp + P * (half + 1))
+                cols = slice(P * half, P * (half + 1))
                 nc.tensor.matmul_mx(
                     out=y_bank[n][:],
-                    lhsT=wq[q][:, cols].bitcast(FP8X4),
-                    lhsT_scale=ws[q][:, cols],
+                    lhsT=wq[q, kp][:, cols].bitcast(FP8X4),
+                    lhsT_scale=ws[q, kp][:, cols],
                     rhs=xq[g, kp][:].bitcast(FP8X4),
                     rhs_scale=xs[g, kp][:],
                     start=(kp == 0),
@@ -192,56 +211,94 @@ def tile_extendedinfomaxicarelativegrad_kernel(tc, x_bytes, x_scale, w, c, k, a,
 
         def y_tanh(n):
             s, g, i = units[n]
-            th[n] = work.tile([P, PASS], F32, name="th", bufs=4, align_bytes=256)
+            th[n] = work.tile([P, PASS], F32, name="th", bufs=5, align_bytes=256)
             nc.scalar.activation(out=th[n][:], in_=y_bank[n][:], func=ACT.Tanh, bias=ck[:, i : i + 1], scale=1.0)
 
-        def elementwise(n):
+        def y_affine(n):
             s, g, i = units[n]
-            tokens = slice(PASS * g, PASS * (g + 1))
-            part = work.tile([P, PASS], F32, name="part", bufs=2, align_bytes=256)
+            if on_gpsimd(n):
+                affine[n] = work.tile([P, PASS], F32, name="affine", bufs=3, align_bytes=256)
+                nc.scalar.activation(
+                    out=affine[n][:], in_=th[n][:], func=ACT.Identity, bias=ck[:, i : i + 1], scale=ck[:, CHUNKS + i : CHUNKS + i + 1]
+                )
+
+        part = {}
+
+        def f_sum(n):
+            s, g, i = units[n]
+            part[n] = work.tile([P, PASS], F32, name="part", bufs=2, align_bytes=256)
+            if on_gpsimd(n):
+                nc.vector.tensor_tensor(out=part[n][:], in0=affine[n][:], in1=y_bank[n][:], op=ALU.add)
+            else:
+                nc.vector.scalar_tensor_tensor(
+                    out=part[n][:], in0=th[n][:], scalar=ck[:, CHUNKS + i : CHUNKS + i + 1], in1=y_bank[n][:], op0=ALU.mult, op1=ALU.add
+                )
+
+        def make_f(n):
+            s, g, i = units[n]
+            a_row = ab_rows[0][:, PASS * g : PASS * (g + 1)]
+            fh_t[n, F] = work.tile([P, PASS], BF16, name="f_t", bufs=3, align_bytes=256)
+            if on_gpsimd(n):
+                nc.gpsimd.tensor_tensor(out=fh_t[n, F][:], in0=part[n][:], in1=a_row, op=ALU.mult)
+            else:
+                nc.vector.scalar_tensor_tensor(
+                    out=fh_t[n, F][:], in0=part[n][:], scalar=ck[:, i : i + 1], in1=a_row, op0=ALU.add, op1=ALU.mult
+                )
+
+        def make_h(n):
+            s, g, i = units[n]
+            b_row = ab_rows[1][:, PASS * g : PASS * (g + 1)]
+            fh_t[n, H] = work.tile([P, PASS], BF16, name="h_t", bufs=3, align_bytes=256)
             nc.vector.scalar_tensor_tensor(
-                out=part[:], in0=th[n][:], scalar=ck[:, CHUNKS + i : CHUNKS + i + 1], in1=y_bank[n][:], op0=ALU.mult, op1=ALU.add
+                out=fh_t[n, H][:], in0=y_bank[n][:], scalar=ck[:, i : i + 1], in1=b_row, op0=ALU.add, op1=ALU.mult
             )
-            h_t[n] = work.tile([P, PASS], BF16, name="h_t", bufs=3, align_bytes=256)
-            nc.vector.scalar_tensor_tensor(
-                out=h_t[n][:], in0=y_bank[n][:], scalar=ck[:, i : i + 1], in1=ab_rows[1][:, tokens], op0=ALU.add, op1=ALU.mult
-            )
-            f_t[n] = work.tile([P, PASS], BF16, name="f_t", bufs=3, align_bytes=256)
-            nc.vector.scalar_tensor_tensor(
-                out=f_t[n][:], in0=part[:], scalar=ck[:, i : i + 1], in1=ab_rows[0][:, tokens], op0=ALU.add, op1=ALU.mult
-            )
+
+        def elementwise(n):
+            f_sum(n)
+            if on_gpsimd(n):
+                make_f(n)
+                make_h(n)
+            else:
+                make_h(n)
+                make_f(n)
 
         turned = {}
+        turns = []
 
-        def turn(n):
-            turned[n] = bank(3 + n % 2)
-            for j, src in enumerate((h_t[n], f_t[n])):
-                words = src[:].bitcast(F32)
+        def turn(items):
+            tb = bank(3 + len(turns) % 2)
+            turns.append(tb)
+            for at, item in enumerate(items):
+                words = fh_t[item][:].bitcast(F32)
+                turned[item] = (tb, at)
                 for u in range(2):
-                    s = 2 * j + u
-                    nc.tensor.transpose(turned[n][:, s * P : (s + 1) * P], words[:, u * P : (u + 1) * P], ident[:])
+                    s = 2 * at + u
+                    nc.tensor.transpose(tb[:, s * P : (s + 1) * P], words[:, u * P : (u + 1) * P], ident[:])
 
-        def regroup(n):
+        def regroup(n, which):
             s, g, i = units[n]
             width = len(STEPS[s])
             place = STEPS[s].index(i)
-            if place == 0:
-                fh_grouped[s, g] = work.tile([P, 2 * width * PASS], BF16, name="fh_grouped", bufs=3, align_bytes=256)
+            if (s, g) not in fh_grouped:
+                fh_grouped[s, g] = work.tile([P, 2 * width * PASS], BF16, name="fh_grouped", bufs=4, align_bytes=256)
             words = fh_grouped[s, g][:].bitcast(F32).rearrange("p (j i m u) -> p j i m u", j=2, i=width, u=2)
-            nc.scalar.copy(out=words[:, :, place, :, :], in_=turned[n][:].rearrange("p (j u m) -> p j m u", j=2, u=2))
+            tb, at = turned[n, which[0]]
+            src = tb[:].rearrange("p (j u m) -> p j m u", j=2, u=2)
+            nc.scalar.copy(out=words[:, which[0] : which[-1] + 1, place, :, :], in_=src[:, at : at + len(which), :, :])
 
-        def fh_quant(n):
+        def fh_quant(n, which):
             s, g, i = units[n]
             if i != STEPS[s][-1]:
                 return
             width = len(STEPS[s])
             cols = slice(P * STEPS[s][0], P * (i + 1))
-            for j, (codes, scales) in enumerate(((hq, hs), (fq, fs))):
+            for j in which:
                 nc.vector.quantize_mx(
-                    out=codes[g][:, cols].bitcast(FP8X4),
-                    scales=scales[g][:, cols],
+                    out=fh_codes[j][g][:, cols].bitcast(FP8X4),
+                    scales=fh_scales[j][g][:, cols],
                     in_=fh_grouped[s, g][:, j * width * PASS : (j + 1) * width * PASS],
                 )
+                quantised[s][j] = g + 1
 
         def sums_of(job):
             sums = []
@@ -266,19 +323,28 @@ def tile_extendedinfomaxicarelativegrad_kernel(tc, x_bytes, x_scale, w, c, k, a,
                 stop=stop,
             )
 
-        def finish(job, acc, on_vector):
+        def diagonal_places(job):
+            return [place + P * row - col0 for row, col0, width, place in sums_of(job) if col0 <= P * row < col0 + width]
+
+        def finish(job, acc):
             result = work.tile([P, 512], F32, name="result", bufs=6, align_bytes=256)
-            if on_vector:
-                nc.vector.tensor_scalar(out=result[:], in0=acc[:], scalar1=-1.0 / ROOT_N, scalar2=None, op0=ALU.mult)
-            else:
-                nc.scalar.activation(out=result[:], in_=acc[:], func=ACT.Copy, scale=-1.0 / ROOT_N)
+            nc.scalar.activation(out=result[:], in_=acc[:], func=ACT.Copy, scale=-1.0 / ROOT_N)
             return result
 
-        def diagonal_and_store(job, result):
-            for row, col0, width, place in sums_of(job):
-                if col0 <= P * row < col0 + width:
-                    at = place + P * row - col0
-                    nc.vector.tensor_tensor(out=result[:, at : at + P], in0=result[:, at : at + P], in1=root_ident[:], op=ALU.add)
+        def finish_on_vector(job, acc):
+            result = work.tile([P, 512], F32, name="result", bufs=6, align_bytes=256)
+            (at,) = diagonal_places(job)
+            nc.vector.tensor_scalar(out=result[:, 0:at], in0=acc[:, 0:at], scalar1=-1.0 / ROOT_N, scalar2=None, op0=ALU.mult)
+            nc.vector.scalar_tensor_tensor(
+                out=result[:, at:], in0=acc[:, at:], scalar=-1.0 / ROOT_N, in1=root_ident[:], op0=ALU.mult, op1=ALU.add
+            )
+            return result
+
+        def add_diagonal(job, result):
+            for at in diagonal_places(job):
+                nc.vector.tensor_tensor(out=result[:, at : at + P], in0=result[:, at : at + P], in1=root_ident[:], op=ALU.add)
+
+        def store(job, result):
             place = 0
             for row0, rows, col0, width in job:
                 nc.sync.dma_start(
@@ -287,85 +353,148 @@ def tile_extendedinfomaxicarelativegrad_kernel(tc, x_bytes, x_scale, w, c, k, a,
                 )
                 place = place + rows * width
 
+        def quantise_x_and_w(j):
+            if j >= 1:
+                w_quant(j - 1)
+            x_quant(j)
+            if j < W_ON_GPSIMD:
+                w_interleave(j)
+
         for h in range(len(x_units)):
             x_unit(h)
             if h % 2 == 1 and h >= 3:
-                x_quant((h - 3) // 2)
-            if h in (1, 3):
-                w_interleave(0, h // 2)
-            if h == 4:
+                quantise_x_and_w((h - 3) // 2)
+            if h == 3:
                 make_ck()
-            if 5 <= h < 9:
-                make_ab(h - 5)
-            if h == 6:
-                w_quant(0)
-            if h in (9, 11):
-                w_interleave(1, (h - 9) // 2)
-            if h in (12, 13):
-                y_matmul(h - 12)
-                y_tanh(h - 12)
+            if 4 <= h < 8:
+                make_ab(h - 4)
+            if h in (9, 11, 13):
+                y_matmul((h - 9) // 2)
+                y_tanh((h - 9) // 2)
+            if h in (12, 14):
+                y_affine(h - 12)
+            if h in (8, 10):
+                w_interleave(W_ON_GPSIMD + (h - 8) // 2)
 
         jobs = [(s, job) for s in range(len(STEPS)) for job in JOBS[s]]
-        quantised = [0] * len(STEPS)
         free_banks = [5, 6, 7]
         accs = []
         passes_done = [0] * len(jobs)
-        n_finished = 0
-        pending = []
+        results = []
 
-        def open_jobs_and_pass():
-            while len(accs) < len(jobs) and free_banks and quantised[jobs[len(accs)][0]] > 0:
+        def groups_ready(j):
+            s, job = jobs[j]
+            new_rows = any(row in STEPS[s] for row, col0, width, place in sums_of(job))
+            return min(quantised[s]) if new_rows else quantised[s][H]
+
+        def open_jobs_and_pass(limit=len(jobs)):
+            while len(accs) < limit and free_banks and groups_ready(len(accs)) > 0:
                 index = free_banks[0]
                 free_banks.remove(index)
                 accs.append((bank(index), index))
-            for j in range(n_finished, len(accs)):
-                s, job = jobs[j]
-                sums = sums_of(job)
-                for g in range(passes_done[j], quantised[s]):
+            for j in range(len(results), min(limit, len(accs))):
+                sums = sums_of(jobs[j][1])
+                for g in range(passes_done[j], groups_ready(j)):
                     for at, one_sum in enumerate(sums):
                         m_pass(accs[j][0], one_sum, g, g == 0 and at == 0, g == GROUPS - 1 and at == len(sums) - 1)
-                passes_done[j] = quantised[s]
+                passes_done[j] = groups_ready(j)
 
-        for n in range(n_units + 1):
-            if n + 2 < n_units:
-                y_matmul(n + 2)
-            if n >= 1:
-                turn(n - 1)
-            if n + 2 < n_units:
-                y_tanh(n + 2)
-            if n >= 1:
-                regroup(n - 1)
+        def finish_next():
+            j = len(results)
+            if passes_done[j] == GROUPS:
+                results.append(finish(jobs[j][1], accs[j][0]))
+                free_banks.append(accs[j][1])
+
+        stored = []
+
+        def store_up_to(count):
+            for j in range(len(stored), count):
+                add_diagonal(jobs[j][1], results[j])
+                store(jobs[j][1], results[j])
+                stored.append(j)
+
+        last = n_units - GROUPS
+        n_quantised = 0
+        n = 0
+        while n < last:
+            batch = [n, n + 1] if on_gpsimd(n) else [n]
+            finished_earlier = len(results)
             open_jobs_and_pass()
-            started = []
-            if passes_done[n_finished] == GROUPS:
-                job = jobs[n_finished][1]
-                started.append((job, finish(job, accs[n_finished][0], False)))
-                free_banks.append(accs[n_finished][1])
-                n_finished = n_finished + 1
-            if n in (4, 6, 12, 14):
-                w_interleave(2 + n // 8, (n % 8 - 4) // 2)
-            if n < n_units:
-                elementwise(n)
-                if n + 3 >= n_units:
-                    free_banks.append(n % 3)
+            for m in batch:
+                elementwise(m)
+                y_matmul(m + 3)
+                finish_next()
+                y_tanh(m + 3)
+            for m in batch:
+                turn([(m, H), (m, F)])
+            if n == 2:
+                w_quant(GROUPS * KP - 1)
+            store_up_to(finished_earlier)
+            for m in range(n_quantised, n):
+                fh_quant(m, BOTH)
+            n_quantised = n
             if n == 0:
-                x_quant(GROUPS * KP - 1)
-            if n in (1, 9, 17):
-                w_quant(1 + n // 8)
-            for job, result in pending:
-                diagonal_and_store(job, result)
-            pending = started
-            if n >= 1:
-                fh_quant(n - 1)
-                s, g, i = units[n - 1]
-                if i == STEPS[s][-1]:
-                    quantised[s] = g + 1
-        for job, result in pending:
-            diagonal_and_store(job, result)
+                quantise_x_and_w(GROUPS * KP - 1)
+            for m in batch:
+                regroup(m, BOTH)
+            for m in batch:
+                y_affine(m + 3)
+            n = n + len(batch)
+
+        u0, u1, u2, u3 = range(last, n_units)
+        strips = len(jobs) - 2
         open_jobs_and_pass()
-        last = list(range(n_finished, len(jobs)))
-        for first in range(0, len(last), 2):
-            both = last[first : first + 2]
-            results = [finish(jobs[j][1], accs[j][0], j % 2 == 1) for j in both]
-            for j, result in zip(both, results):
-                diagonal_and_store(jobs[j][1], result)
+        f_sum(u0)
+        make_h(u0)
+        y_matmul(u3)
+        finish_next()
+        y_tanh(u3)
+        make_h(u1)
+        make_f(u0)
+        store_up_to(len(results))
+        fh_quant(u0 - 1, BOTH)
+        turn([(u0, H), (u0, F)])
+        regroup(u0, BOTH)
+        open_jobs_and_pass()
+        finish_next()
+        f_sum(u1)
+        free_banks.append(u1 % 3)
+        make_h(u2)
+        turn([(u1, H), (u2, H)])
+        regroup(u1, (H,))
+        regroup(u2, (H,))
+        finish_next()
+        make_f(u1)
+        make_h(u3)
+        fh_quant(u0, BOTH)
+        turn([(u1, F), (u3, H)])
+        regroup(u3, (H,))
+        regroup(u1, (F,))
+        finish_next()
+        store_up_to(len(results))
+        open_jobs_and_pass(strips + 1)
+        f_sum(u2)
+        fh_quant(u1, (H,))
+        fh_quant(u2, (H,))
+        open_jobs_and_pass(strips)
+        make_f(u2)
+        turn([(u2, F)])
+        regroup(u2, (F,))
+        open_jobs_and_pass()
+        f_sum(u3)
+        fh_quant(u3, (H,))
+        fh_quant(u1, (F,))
+        open_jobs_and_pass(strips)
+        make_f(u3)
+        turn([(u3, F)])
+        finish_next()
+        regroup(u3, (F,))
+        open_jobs_and_pass()
+        fh_quant(u2, (F,))
+        open_jobs_and_pass()
+        finish_next()
+        fh_quant(u3, (F,))
+        open_jobs_and_pass()
+        store_up_to(len(results))
+        store(jobs[strips][1], finish_on_vector(jobs[strips][1], accs[strips][0]))
+        store(jobs[strips + 1][1], finish(jobs[strips + 1][1], accs[strips + 1][0]))

@@ -23,14 +23,15 @@ KP = D // PASS
 CHUNKS = M // P
 ROOT_N = math.sqrt(N)
 
-SHARED_UNITS = 24
-W_ON_GPSIMD = 6
+SHARED_UNITS = 28
+W_ON_GPSIMD = 4
 H, F = 0, 1
 BOTH = (H, F)
-STEPS = [(0, 1), (2, 3), (4,), (5,), (6,), (7,)]
+X_ALONE = 8
+MIXED = 16 - X_ALONE
+STEPS = [(0, 1, 2, 3), (4,), (5,), (6,), (7,)]
 JOBS = [
-    [[(0, 2, 0, 256)]],
-    [[(2, 1, 0, 512)], [(3, 1, 0, 512)], [(0, 2, 256, 256)]],
+    [[(0, 1, 0, 512)], [(1, 1, 0, 512)], [(2, 1, 0, 512)], [(3, 1, 0, 512)]],
     [[(4, 1, 0, 512)], [(0, 4, 512, 128)]],
     [[(5, 1, 0, 512)], [(0, 4, 640, 128)], [(4, 2, 512, 256)]],
     [[(6, 1, 0, 512)], [(0, 4, 768, 128)], [(6, 1, 512, 256), (4, 2, 768, 128)]],
@@ -49,6 +50,18 @@ def tile_extendedinfomaxicarelativegrad_kernel(tc, x_bytes, x_scale, w, c, k, a,
         def bank(index, dtype=F32):
             width = 512 if dtype == F32 else 1024
             return psum.tile([P, width], dtype, name="bank%d" % index, tag="bank%d" % index)
+
+        turn_banks = [2, 3, 4]
+        y_banks = [0, 1]
+
+        def rotate(indices):
+            index = indices[0]
+            indices.remove(index)
+            indices.append(index)
+            return index
+
+        def turn_bank():
+            return bank(rotate(turn_banks))
 
         ident = keep.tile([P, P], F32, name="ident", align_bytes=64)
         make_identity(nc, ident[:])
@@ -79,7 +92,6 @@ def tile_extendedinfomaxicarelativegrad_kernel(tc, x_bytes, x_scale, w, c, k, a,
 
         load_x(0)
         load_w(0)
-        load_x(1)
         nc.sync.dma_start(out=ck_rows[0:CHUNKS, :], in_=c.rearrange("(i p) -> i p", p=P))
         nc.sync.dma_start(out=ck_rows[CHUNKS : 2 * CHUNKS, :], in_=k.rearrange("(i p) -> i p", p=P))
         ab_cols = []
@@ -87,9 +99,10 @@ def tile_extendedinfomaxicarelativegrad_kernel(tc, x_bytes, x_scale, w, c, k, a,
             cols = keep.tile([P, 16], BF16, name=name, align_bytes=64)
             nc.sync.dma_start(out=cols[:], in_=vec.rearrange("(n j) -> n j", j=16))
             ab_cols.append(cols)
+        load_x(1)
         load_w(1)
-        load_x(2)
         load_w(2)
+        load_x(2)
         load_x(3)
         load_w(3)
 
@@ -105,7 +118,9 @@ def tile_extendedinfomaxicarelativegrad_kernel(tc, x_bytes, x_scale, w, c, k, a,
         xq = {}
         xs = {}
 
-        def x_unit(h):
+        x_scaled = {}
+
+        def x_scale_unit(h):
             g, kp, u = x_units[h]
             scaled = work.tile([P, 2, PASS], BF16, name="x_scaled", bufs=4, align_bytes=256)
             for e in range(2):
@@ -115,8 +130,12 @@ def tile_extendedinfomaxicarelativegrad_kernel(tc, x_bytes, x_scale, w, c, k, a,
                     in1=scale_bank[kp][:],
                     op=ALU.mult,
                 )
-            words = scaled[:].rearrange("p e d -> p (e d)").bitcast(F32)
-            tb = bank((3, 4, 7)[h % 3])
+            x_scaled[h] = scaled
+
+        def x_turn(h):
+            g, kp, u = x_units[h]
+            words = x_scaled[h][:].rearrange("p e d -> p (e d)").bitcast(F32)
+            tb = turn_bank()
             for e in range(2):
                 for v in range(2):
                     s = 2 * e + v
@@ -137,17 +156,23 @@ def tile_extendedinfomaxicarelativegrad_kernel(tc, x_bytes, x_scale, w, c, k, a,
 
         w_grouped = {}
 
-        def w_interleave(j):
-            q, kp = divmod(j, KP)
-            src = w_raw[q, kp][:].rearrange("p t m -> p m t")
-            if j < W_ON_GPSIMD:
-                w_grouped[j] = x_grouped[divmod(j, KP)][:, 0:1024]
-                dst = w_grouped[j].rearrange("p (m t) -> p m t", t=4)
-                nc.gpsimd.tensor_scalar(out=dst, in0=src, scalar1=1.0, scalar2=0.0, op0=ALU.mult, op1=ALU.add)
-            else:
-                own = keep.tile([P, 1024], BF16, name="w_grouped%d" % j, align_bytes=256)
-                w_grouped[j] = own[:]
-                nc.scalar.copy(out=w_grouped[j].rearrange("p (m t) -> p m t", t=4), in_=src)
+        def w_interleave_gpsimd(j, dst):
+            w_grouped[j] = dst
+            src = w_raw[divmod(j, KP)][:].rearrange("p t m -> p m t")
+            nc.gpsimd.tensor_scalar(
+                out=dst.rearrange("p (m t) -> p m t", t=4), in0=src, scalar1=1.0, scalar2=0.0, op0=ALU.mult, op1=ALU.add
+            )
+
+        def w_own_tile(j):
+            own = keep.tile([P, 1024], BF16, name="w_grouped%d" % j, align_bytes=256)
+            return own[:]
+
+        def w_interleave_scalar(j, half):
+            if half == 0:
+                w_grouped[j] = w_own_tile(j)
+            src = w_raw[divmod(j, KP)][:, :, P * half : P * (half + 1)].rearrange("p t m -> p m t")
+            dst = w_grouped[j][:, PASS * half : PASS * (half + 1)]
+            nc.scalar.copy(out=dst.rearrange("p (m t) -> p m t", t=4), in_=src)
 
         def w_quant(j):
             q, kp = divmod(j, KP)
@@ -158,7 +183,7 @@ def tile_extendedinfomaxicarelativegrad_kernel(tc, x_bytes, x_scale, w, c, k, a,
         ck = keep.tile([P, 2 * CHUNKS], F32, name="ck", align_bytes=64)
 
         def make_ck():
-            cb = bank(0, BF16)
+            cb = bank(7, BF16)
             nc.tensor.transpose(cb[:, 0:P], ck_rows[:], ident_bf[:])
             nc.scalar.copy(out=ck[:], in_=cb[:, 0 : 2 * CHUNKS])
 
@@ -166,7 +191,7 @@ def tile_extendedinfomaxicarelativegrad_kernel(tc, x_bytes, x_scale, w, c, k, a,
 
         def make_ab(j):
             which, u = divmod(j, 2)
-            sb = bank((1, 2, 0, 1)[j])
+            sb = bank((0, 1, 7, 0)[j])
             words = ab_cols[which][:].bitcast(F32)
             for r in range(4):
                 col = 2 * r + u
@@ -177,6 +202,7 @@ def tile_extendedinfomaxicarelativegrad_kernel(tc, x_bytes, x_scale, w, c, k, a,
         units = [(s, g, i) for s, chunks in enumerate(STEPS) for g in range(GROUPS) for i in chunks]
         n_units = len(units)
         y_bank = {}
+        y_index = {}
         th = {}
         fh_t = {}
         quantised = [[0, 0] for s in STEPS]
@@ -191,12 +217,13 @@ def tile_extendedinfomaxicarelativegrad_kernel(tc, x_bytes, x_scale, w, c, k, a,
         affine = {}
 
         def on_gpsimd(n):
-            return n % 2 == 0 and n < SHARED_UNITS
+            return n < MIXED or ((n - MIXED) % 2 == 0 and n + 1 < SHARED_UNITS)
 
         def y_matmul(n):
             s, g, i = units[n]
             q, half = divmod(i, 2)
-            y_bank[n] = bank(n % 3)
+            y_index[n] = rotate(y_banks)
+            y_bank[n] = bank(y_index[n])
             for kp in range(KP):
                 cols = slice(P * half, P * (half + 1))
                 nc.tensor.matmul_mx(
@@ -263,11 +290,9 @@ def tile_extendedinfomaxicarelativegrad_kernel(tc, x_bytes, x_scale, w, c, k, a,
                 make_f(n)
 
         turned = {}
-        turns = []
 
         def turn(items):
-            tb = bank(3 + len(turns) % 2)
-            turns.append(tb)
+            tb = turn_bank()
             for at, item in enumerate(items):
                 words = fh_t[item][:].bitcast(F32)
                 turned[item] = (tb, at)
@@ -353,31 +378,8 @@ def tile_extendedinfomaxicarelativegrad_kernel(tc, x_bytes, x_scale, w, c, k, a,
                 )
                 place = place + rows * width
 
-        def quantise_x_and_w(j):
-            if j >= 1:
-                w_quant(j - 1)
-            x_quant(j)
-            if j < W_ON_GPSIMD:
-                w_interleave(j)
-
-        for h in range(len(x_units)):
-            x_unit(h)
-            if h % 2 == 1 and h >= 3:
-                quantise_x_and_w((h - 3) // 2)
-            if h == 3:
-                make_ck()
-            if 4 <= h < 8:
-                make_ab(h - 4)
-            if h in (9, 11, 13):
-                y_matmul((h - 9) // 2)
-                y_tanh((h - 9) // 2)
-            if h in (12, 14):
-                y_affine(h - 12)
-            if h in (8, 10):
-                w_interleave(W_ON_GPSIMD + (h - 8) // 2)
-
         jobs = [(s, job) for s in range(len(STEPS)) for job in JOBS[s]]
-        free_banks = [5, 6, 7]
+        free_banks = [7]
         accs = []
         passes_done = [0] * len(jobs)
         results = []
@@ -413,30 +415,94 @@ def tile_extendedinfomaxicarelativegrad_kernel(tc, x_bytes, x_scale, w, c, k, a,
                 store(jobs[j][1], results[j])
                 stored.append(j)
 
+        for j in range(KP):
+            w_interleave_gpsimd(j, w_own_tile(j))
+        for h in range(X_ALONE):
+            x_scale_unit(h)
+            if h >= 6:
+                y_affine(h - 6)
+            if h in (4, 5):
+                w_interleave_scalar(W_ON_GPSIMD, h - 4)
+            x_turn(h)
+            if h == 0:
+                make_ck()
+            if h < 4:
+                make_ab(h)
+            if h == 3:
+                w_quant(0)
+                w_quant(1)
+                x_quant(0)
+                w_interleave_gpsimd(2, x_grouped[0, 0][:, 0:1024])
+            if h == 5:
+                w_quant(2)
+                x_quant(1)
+                w_interleave_gpsimd(3, x_grouped[0, 1][:, 0:1024])
+            if h in (5, 6):
+                y_matmul(h - 5)
+                y_tanh(h - 5)
+            if h == 7:
+                w_quant(3)
+                x_quant(2)
+
+        x_done = KP + 1
+        for n in range(MIXED):
+            h = X_ALONE + n
+            elementwise(n)
+            y_matmul(n + 2)
+            y_tanh(n + 2)
+            x_scale_unit(h)
+            if 2 * x_done + 1 < h:
+                x_quant(x_done)
+                x_done = x_done + 1
+            if n >= 1:
+                fh_quant(n - 1, BOTH)
+            if n in (3, 5):
+                w_quant(W_ON_GPSIMD + (n - 3) // 2)
+            turn([(n, H), (n, F)])
+            regroup(n, BOTH)
+            x_turn(h)
+            open_jobs_and_pass()
+            y_affine(n + 2)
+            if n < 6:
+                w_interleave_scalar(W_ON_GPSIMD + 1 + n // 2, n % 2)
+        n_quantised = MIXED - 1
+        turn_banks.remove(2)
+        y_banks.remove(y_index[MIXED])
+        y_banks.remove(y_index[MIXED + 1])
+        y_banks.extend([2, y_index[MIXED], y_index[MIXED + 1]])
+        free_banks.extend([5, 6])
+        y_matmul(MIXED + 2)
+        y_tanh(MIXED + 2)
+        y_affine(MIXED + 2)
+
         last = n_units - GROUPS
-        n_quantised = 0
-        n = 0
+        n = MIXED
         while n < last:
             batch = [n, n + 1] if on_gpsimd(n) else [n]
             finished_earlier = len(results)
             open_jobs_and_pass()
             for m in batch:
                 elementwise(m)
-                y_matmul(m + 3)
-                finish_next()
-                y_tanh(m + 3)
+                if (units[m + 3][1], KP - 1) in xq:
+                    y_matmul(m + 3)
+                    finish_next()
+                    y_tanh(m + 3)
             for m in batch:
                 turn([(m, H), (m, F)])
-            if n == 2:
-                w_quant(GROUPS * KP - 1)
             store_up_to(finished_earlier)
             for m in range(n_quantised, n):
                 fh_quant(m, BOTH)
             n_quantised = n
-            if n == 0:
-                quantise_x_and_w(GROUPS * KP - 1)
+            if n == 18:
+                w_quant(6)
+                w_quant(7)
+            if n == MIXED:
+                x_quant(GROUPS * KP - 1)
+                y_matmul(n + 4)
             for m in batch:
                 regroup(m, BOTH)
+            if n == MIXED:
+                y_tanh(n + 4)
             for m in batch:
                 y_affine(m + 3)
             n = n + len(batch)
@@ -451,18 +517,21 @@ def tile_extendedinfomaxicarelativegrad_kernel(tc, x_bytes, x_scale, w, c, k, a,
         y_tanh(u3)
         make_h(u1)
         make_f(u0)
-        store_up_to(len(results))
-        fh_quant(u0 - 1, BOTH)
         turn([(u0, H), (u0, F)])
         regroup(u0, BOTH)
         open_jobs_and_pass()
+        for m in range(n_quantised, u0):
+            fh_quant(m, BOTH)
+        open_jobs_and_pass(strips - 3)
         finish_next()
         f_sum(u1)
-        free_banks.append(u1 % 3)
+        free_banks.append(y_index[u1])
         make_h(u2)
+        store_up_to(len(results))
         turn([(u1, H), (u2, H)])
         regroup(u1, (H,))
         regroup(u2, (H,))
+        open_jobs_and_pass(strips - 2)
         finish_next()
         make_f(u1)
         make_h(u3)
@@ -472,27 +541,27 @@ def tile_extendedinfomaxicarelativegrad_kernel(tc, x_bytes, x_scale, w, c, k, a,
         regroup(u1, (F,))
         finish_next()
         store_up_to(len(results))
-        open_jobs_and_pass(strips + 1)
+        open_jobs_and_pass(strips)
         f_sum(u2)
         fh_quant(u1, (H,))
         fh_quant(u2, (H,))
-        open_jobs_and_pass(strips)
+        open_jobs_and_pass(strips - 1)
         make_f(u2)
         turn([(u2, F)])
         regroup(u2, (F,))
-        open_jobs_and_pass()
+        open_jobs_and_pass(strips)
         f_sum(u3)
         fh_quant(u3, (H,))
         fh_quant(u1, (F,))
-        open_jobs_and_pass(strips)
+        open_jobs_and_pass(strips - 1)
         make_f(u3)
         turn([(u3, F)])
-        finish_next()
         regroup(u3, (F,))
-        open_jobs_and_pass()
+        finish_next()
+        open_jobs_and_pass(strips)
+        finish_next()
         fh_quant(u2, (F,))
         open_jobs_and_pass()
-        finish_next()
         fh_quant(u3, (F,))
         open_jobs_and_pass()
         store_up_to(len(results))

@@ -10,6 +10,7 @@ FLOPS = 2 * N * D * M + 2 * N * M * M
 F32 = mybir.dt.float32
 BF16 = mybir.dt.bfloat16
 U32 = mybir.dt.uint32
+I32 = mybir.dt.int32
 U8 = mybir.dt.uint8
 FP8 = mybir.dt.float8_e4m3fn
 FP8X4 = mybir.dt.float8_e4m3fn_x4
@@ -28,6 +29,7 @@ W_ON_GPSIMD = 4
 H, F = 0, 1
 BOTH = (H, F)
 X_ALONE = 8
+AB_AT = (0, 1, 3, 4)
 MIXED = 16 - X_ALONE
 STEPS = [(0, 1, 2, 3), (4,), (5,), (6,), (7,)]
 JOBS = [
@@ -72,6 +74,9 @@ def tile_extendedinfomaxicarelativegrad_kernel(tc, x_bytes, x_scale, w, c, k, a,
         root_ident = keep.tile([P, P], F32, name="root_ident", align_bytes=64)
         nc.gpsimd.tensor_scalar(out=root_ident[:], in0=ident[:], scalar1=ROOT_N, scalar2=0.0, op0=ALU.mult, op1=ALU.add)
 
+        ab_first = keep.tile([P, N], BF16, name="ab_first", align_bytes=256)
+        nc.vector.memset(ab_first[:].bitcast(I32), 0)
+
         scale_cols = keep.tile([P, KP, 4], F32, name="scale_cols", align_bytes=64)
         nc.sync.dma_start(out=scale_cols[:], in_=x_scale.rearrange("o (g p t) -> p (o g) t", p=P, t=4))
 
@@ -94,24 +99,25 @@ def tile_extendedinfomaxicarelativegrad_kernel(tc, x_bytes, x_scale, w, c, k, a,
         load_w(0)
         nc.sync.dma_start(out=ck_rows[0:CHUNKS, :], in_=c.rearrange("(i p) -> i p", p=P))
         nc.sync.dma_start(out=ck_rows[CHUNKS : 2 * CHUNKS, :], in_=k.rearrange("(i p) -> i p", p=P))
-        ab_cols = []
-        for name, vec in (("a_cols", a), ("b_cols", b)):
-            cols = keep.tile([P, 16], BF16, name=name, align_bytes=64)
-            nc.sync.dma_start(out=cols[:], in_=vec.rearrange("(n j) -> n j", j=16))
-            ab_cols.append(cols)
-        load_x(1)
+        nc.sync.dma_start(out=ab_first[0:1, :], in_=a.rearrange("(o n) -> o n", o=1))
+        nc.sync.dma_start(out=ab_first[1:2, :], in_=b.rearrange("(o n) -> o n", o=1))
         load_w(1)
+        load_x(1)
         load_w(2)
         load_x(2)
         load_x(3)
         load_w(3)
 
         scale_bank = []
-        for kp in range(KP):
+
+        def spread_scale(kp):
             sb = bank(5 + kp)
             for t in range(4):
                 nc.tensor.transpose(sb[:, t:512:4], scale_cols[:, kp, t : t + 1].to_broadcast([P, P]), ident[:])
             scale_bank.append(sb)
+
+        spread_scale(0)
+        spread_scale(1)
 
         x_units = [(g, kp, u) for g in range(GROUPS) for kp in range(KP) for u in range(2)]
         x_grouped = {}
@@ -190,14 +196,18 @@ def tile_extendedinfomaxicarelativegrad_kernel(tc, x_bytes, x_scale, w, c, k, a,
         ab_rows = [keep.tile([P, N], BF16, name="a_rows", align_bytes=256), keep.tile([P, N], BF16, name="b_rows", align_bytes=256)]
 
         def make_ab(j):
-            which, u = divmod(j, 2)
-            sb = bank((0, 1, 7, 0)[j])
-            words = ab_cols[which][:].bitcast(F32)
-            for r in range(4):
-                col = 2 * r + u
-                nc.tensor.transpose(sb[:, r * P : (r + 1) * P], words[:, col : col + 1].to_broadcast([P, P]), ident[:])
-            dst = ab_rows[which][:].bitcast(F32).rearrange("p (g u s r) -> p g u s r", g=GROUPS, u=2, r=4)[:, :, u, :, :]
-            nc.scalar.copy(out=dst, in_=sb[:].rearrange("p (r g s) -> p g s r", r=4, g=GROUPS))
+            half, which = divmod(j, 2)
+            sb = bank((0, 1, 7, 7)[j], BF16)
+            for at in range(2):
+                g = 2 * half + at
+                nc.tensor.matmul(
+                    out=sb[:, PASS * at : PASS * (at + 1)].rearrange("m (u p e) -> m u p e", u=2, e=2),
+                    lhsT=ident_bf[:, which : which + 1].to_broadcast([P, P]),
+                    rhs=ab_first[:, PASS * g : PASS * (g + 1)].rearrange("r (p u e) -> r u p e", u=2, e=2),
+                    start=True,
+                    stop=True,
+                )
+            nc.scalar.copy(out=ab_rows[which][:, 2 * PASS * half : 2 * PASS * (half + 1)], in_=sb[:])
 
         units = [(s, g, i) for s, chunks in enumerate(STEPS) for g in range(GROUPS) for i in chunks]
         n_units = len(units)
@@ -305,7 +315,7 @@ def tile_extendedinfomaxicarelativegrad_kernel(tc, x_bytes, x_scale, w, c, k, a,
             width = len(STEPS[s])
             place = STEPS[s].index(i)
             if (s, g) not in fh_grouped:
-                fh_grouped[s, g] = work.tile([P, 2 * width * PASS], BF16, name="fh_grouped", bufs=4, align_bytes=256)
+                fh_grouped[s, g] = work.tile([P, 2 * width * PASS], BF16, name="fh_grouped", bufs=3, align_bytes=256)
             words = fh_grouped[s, g][:].bitcast(F32).rearrange("p (j i m u) -> p j i m u", j=2, i=width, u=2)
             tb, at = turned[n, which[0]]
             src = tb[:].rearrange("p (j u m) -> p j m u", j=2, u=2)
@@ -415,7 +425,7 @@ def tile_extendedinfomaxicarelativegrad_kernel(tc, x_bytes, x_scale, w, c, k, a,
                 store(jobs[j][1], results[j])
                 stored.append(j)
 
-        for j in range(KP):
+        for j in range(3):
             w_interleave_gpsimd(j, w_own_tile(j))
         for h in range(X_ALONE):
             x_scale_unit(h)
@@ -424,17 +434,15 @@ def tile_extendedinfomaxicarelativegrad_kernel(tc, x_bytes, x_scale, w, c, k, a,
             if h in (4, 5):
                 w_interleave_scalar(W_ON_GPSIMD, h - 4)
             x_turn(h)
-            if h == 0:
+            if h == 1:
                 make_ck()
-            if h < 4:
-                make_ab(h)
-            if h == 3:
-                w_quant(0)
-                w_quant(1)
+            if h in AB_AT:
+                make_ab(AB_AT.index(h))
+            if h == 4:
+                for j in range(3):
+                    w_quant(j)
                 x_quant(0)
-                w_interleave_gpsimd(2, x_grouped[0, 0][:, 0:1024])
             if h == 5:
-                w_quant(2)
                 x_quant(1)
                 w_interleave_gpsimd(3, x_grouped[0, 1][:, 0:1024])
             if h in (5, 6):
@@ -450,22 +458,22 @@ def tile_extendedinfomaxicarelativegrad_kernel(tc, x_bytes, x_scale, w, c, k, a,
             elementwise(n)
             y_matmul(n + 2)
             y_tanh(n + 2)
+            if n < 6:
+                w_interleave_scalar(W_ON_GPSIMD + 1 + n // 2, n % 2)
+            y_affine(n + 2)
             x_scale_unit(h)
-            if 2 * x_done + 1 < h:
+            if 2 * x_done + 2 < h:
                 x_quant(x_done)
                 x_done = x_done + 1
-            if n >= 1:
-                fh_quant(n - 1, BOTH)
+            if n >= 2:
+                fh_quant(n - 2, BOTH)
             if n in (3, 5):
                 w_quant(W_ON_GPSIMD + (n - 3) // 2)
             turn([(n, H), (n, F)])
             regroup(n, BOTH)
             x_turn(h)
             open_jobs_and_pass()
-            y_affine(n + 2)
-            if n < 6:
-                w_interleave_scalar(W_ON_GPSIMD + 1 + n // 2, n % 2)
-        n_quantised = MIXED - 1
+        n_quantised = MIXED - 2
         turn_banks.remove(2)
         y_banks.remove(y_index[MIXED])
         y_banks.remove(y_index[MIXED + 1])

@@ -20,25 +20,31 @@ ACT = mybir.ActivationFunctionType
 P = 128
 PASS = 512
 GROUPS = N // PASS
-KP = D // PASS
+D_PASSES = D // PASS
 CHUNKS = M // P
+W_COLS = 256
 ROOT_N = math.sqrt(N)
-
-SHARED_UNITS = 28
-W_ON_GPSIMD = 4
 H, F = 0, 1
 BOTH = (H, F)
+
+X_PARTS = GROUPS * D_PASSES * 2
 X_ALONE = 8
-AB_AT = (0, 1, 3, 4)
-MIXED = 16 - X_ALONE
+MIXED = X_PARTS - X_ALONE
+W_ON_GPSIMD = 4
+AB_SECOND_HALF = 3
+
 STEPS = [(0, 1, 2, 3), (4,), (5,), (6,), (7,)]
 JOBS = [
     [[(0, 1, 0, 512)], [(1, 1, 0, 512)], [(2, 1, 0, 512)], [(3, 1, 0, 512)]],
     [[(4, 1, 0, 512)], [(0, 4, 512, 128)]],
     [[(5, 1, 0, 512)], [(0, 4, 640, 128)], [(4, 2, 512, 256)]],
     [[(6, 1, 0, 512)], [(0, 4, 768, 128)], [(6, 1, 512, 256), (4, 2, 768, 128)]],
-    [[(0, 4, 896, 128)], [(6, 1, 768, 256), (4, 2, 896, 128)], [(7, 1, 512, 512)], [(7, 1, 0, 512)]],
+    [[(0, 4, 896, 128)], [(6, 1, 768, 256), (4, 2, 896, 128)], [(7, 1, 512, 512)], [(7, 1, 0, 256)], [(7, 1, 256, 256)]],
 ]
+
+SCALE_BANKS = (5, 6)
+SETUP_BANK = 7
+THIRD_UNIT_BANK = 2
 
 
 def tile_extendedinfomaxicarelativegrad_kernel(tc, x_bytes, x_scale, w, c, k, a, b, out):
@@ -50,20 +56,17 @@ def tile_extendedinfomaxicarelativegrad_kernel(tc, x_bytes, x_scale, w, c, k, a,
         ctx.enter_context(tc.manual_schedule())
 
         def bank(index, dtype=F32):
-            width = 512 if dtype == F32 else 1024
-            return psum.tile([P, width], dtype, name="bank%d" % index, tag="bank%d" % index)
+            return psum.tile([P, PASS if dtype == F32 else 2 * PASS], dtype, name="bank%d" % index, tag="bank%d" % index)
 
-        turn_banks = [2, 3, 4]
-        y_banks = [0, 1]
+        turn_banks = [THIRD_UNIT_BANK, 3, 4]
+        unit_banks = [0, 1]
+        free_job_banks = [SETUP_BANK]
 
         def rotate(indices):
             index = indices[0]
             indices.remove(index)
             indices.append(index)
             return index
-
-        def turn_bank():
-            return bank(rotate(turn_banks))
 
         ident = keep.tile([P, P], F32, name="ident", align_bytes=64)
         make_identity(nc, ident[:])
@@ -73,34 +76,34 @@ def tile_extendedinfomaxicarelativegrad_kernel(tc, x_bytes, x_scale, w, c, k, a,
         make_identity(nc, ident_bf[:])
         root_ident = keep.tile([P, P], F32, name="root_ident", align_bytes=64)
         nc.gpsimd.tensor_scalar(out=root_ident[:], in0=ident[:], scalar1=ROOT_N, scalar2=0.0, op0=ALU.mult, op1=ALU.add)
+        ab_loaded = keep.tile([P, N], BF16, name="ab_loaded", align_bytes=256)
+        nc.vector.memset(ab_loaded[:].bitcast(I32), 0)
 
-        ab_first = keep.tile([P, N], BF16, name="ab_first", align_bytes=256)
-        nc.vector.memset(ab_first[:].bitcast(I32), 0)
-
-        scale_cols = keep.tile([P, KP, 4], F32, name="scale_cols", align_bytes=64)
+        scale_cols = keep.tile([P, D_PASSES, 4], F32, name="scale_cols", align_bytes=64)
         nc.sync.dma_start(out=scale_cols[:], in_=x_scale.rearrange("o (g p t) -> p (o g) t", p=P, t=4))
 
         x_view = x_bytes.rearrange("(g q j) d -> g q j d", q=P, j=4)
         w_view = w.rearrange("(g p t) m -> g p t m", p=P, t=4)
-        xb = {}
+        x_raw = {}
         w_raw = {}
 
         def load_x(g):
             for u in range(2):
-                xb[g, u] = keep.tile([P, 2, D], U8, name="xbytes%d%d" % (g, u), align_bytes=256)
-                nc.sync.dma_start(out=xb[g, u][:], in_=x_view[g, :, 2 * u : 2 * u + 2, :])
+                x_raw[g, u] = keep.tile([P, 2, D], U8, name="xbytes%d%d" % (g, u), align_bytes=256)
+                nc.sync.dma_start(out=x_raw[g, u][:], in_=x_view[g, :, 2 * u : 2 * u + 2, :])
 
-        def load_w(q):
-            for kp in range(KP):
-                w_raw[q, kp] = keep.tile([P, 4, 256], BF16, name="wraw%d%d" % (q, kp), align_bytes=256)
-                nc.sync.dma_start(out=w_raw[q, kp][:], in_=w_view[kp, :, :, 256 * q : 256 * (q + 1)])
+        def load_w(quarter):
+            for dp in range(D_PASSES):
+                piece = D_PASSES * quarter + dp
+                w_raw[piece] = keep.tile([P, 4, W_COLS], BF16, name="wraw%d" % piece, align_bytes=256)
+                nc.sync.dma_start(out=w_raw[piece][:], in_=w_view[dp, :, :, W_COLS * quarter : W_COLS * (quarter + 1)])
 
         load_x(0)
         load_w(0)
         nc.sync.dma_start(out=ck_rows[0:CHUNKS, :], in_=c.rearrange("(i p) -> i p", p=P))
         nc.sync.dma_start(out=ck_rows[CHUNKS : 2 * CHUNKS, :], in_=k.rearrange("(i p) -> i p", p=P))
-        nc.sync.dma_start(out=ab_first[0:1, :], in_=a.rearrange("(o n) -> o n", o=1))
-        nc.sync.dma_start(out=ab_first[1:2, :], in_=b.rearrange("(o n) -> o n", o=1))
+        nc.sync.dma_start(out=ab_loaded[0:1, :], in_=a.rearrange("(o n) -> o n", o=1))
+        nc.sync.dma_start(out=ab_loaded[1:2, :], in_=b.rearrange("(o n) -> o n", o=1))
         load_w(1)
         load_x(1)
         load_w(2)
@@ -108,190 +111,183 @@ def tile_extendedinfomaxicarelativegrad_kernel(tc, x_bytes, x_scale, w, c, k, a,
         load_x(3)
         load_w(3)
 
-        scale_bank = []
-
-        def spread_scale(kp):
-            sb = bank(5 + kp)
+        scale_rows = []
+        for dp in range(D_PASSES):
+            scale_rows.append(bank(SCALE_BANKS[dp]))
             for t in range(4):
-                nc.tensor.transpose(sb[:, t:512:4], scale_cols[:, kp, t : t + 1].to_broadcast([P, P]), ident[:])
-            scale_bank.append(sb)
+                nc.tensor.transpose(scale_rows[dp][:, t:PASS:4], scale_cols[:, dp, t : t + 1].to_broadcast([P, P]), ident[:])
 
-        spread_scale(0)
-        spread_scale(1)
-
-        x_units = [(g, kp, u) for g in range(GROUPS) for kp in range(KP) for u in range(2)]
-        x_grouped = {}
-        xq = {}
-        xs = {}
-
+        x_parts = [(g, dp, u) for g in range(GROUPS) for dp in range(D_PASSES) for u in range(2)]
         x_scaled = {}
+        x_grouped = {}
+        x_codes = {}
+        x_scales = {}
 
-        def x_scale_unit(h):
-            g, kp, u = x_units[h]
-            scaled = work.tile([P, 2, PASS], BF16, name="x_scaled", bufs=4, align_bytes=256)
+        def x_widen(part):
+            g, dp, u = x_parts[part]
+            x_scaled[part] = work.tile([P, 2, PASS], BF16, name="x_scaled", bufs=4, align_bytes=256)
             for e in range(2):
                 nc.vector.tensor_tensor(
-                    out=scaled[:, e, :],
-                    in0=xb[g, u][:, e, kp * PASS : (kp + 1) * PASS].bitcast(FP8),
-                    in1=scale_bank[kp][:],
+                    out=x_scaled[part][:, e, :],
+                    in0=x_raw[g, u][:, e, dp * PASS : (dp + 1) * PASS].bitcast(FP8),
+                    in1=scale_rows[dp][:],
                     op=ALU.mult,
                 )
-            x_scaled[h] = scaled
 
-        def x_turn(h):
-            g, kp, u = x_units[h]
-            words = x_scaled[h][:].rearrange("p e d -> p (e d)").bitcast(F32)
-            tb = turn_bank()
+        def x_turn(part):
+            g, dp, u = x_parts[part]
+            words = x_scaled[part][:].rearrange("p e d -> p (e d)").bitcast(F32)
+            turned_x = bank(rotate(turn_banks))
             for e in range(2):
                 for v in range(2):
-                    s = 2 * e + v
-                    nc.tensor.transpose(tb[:, s * P : (s + 1) * P], words[:, 256 * e + v : 256 * (e + 1) : 2], ident[:])
+                    at = P * (2 * e + v)
+                    nc.tensor.transpose(turned_x[:, at : at + P], words[:, 256 * e + v : 256 * (e + 1) : 2], ident[:])
             if u == 0:
-                x_grouped[g, kp] = work.tile([P, 4 * PASS], BF16, name="x_grouped", bufs=4, align_bytes=256)
-            dst = x_grouped[g, kp][:].bitcast(F32)[:, 512 * u : 512 * (u + 1)]
-            nc.scalar.copy(out=dst.rearrange("p (q s) -> p q s", s=4), in_=tb[:].rearrange("p (s q) -> p q s", s=4))
+                x_grouped[g, dp] = work.tile([P, 4 * PASS], BF16, name="x_grouped", bufs=4, align_bytes=256)
+            dst = x_grouped[g, dp][:].bitcast(F32)[:, PASS * u : PASS * (u + 1)]
+            nc.scalar.copy(out=dst.rearrange("p (q s) -> p q s", s=4), in_=turned_x[:].rearrange("p (s q) -> p q s", s=4))
 
-        def x_quant(j):
-            g, kp = divmod(j, KP)
-            xq[g, kp] = keep.tile([P, PASS], U32, name="xq%d" % j, align_bytes=256)
-            xs[g, kp] = keep.tile([P, PASS], U8, name="xs%d" % j, align_bytes=256)
-            nc.vector.quantize_mx(out=xq[g, kp][:].bitcast(FP8X4), scales=xs[g, kp][:], in_=x_grouped[g, kp][:])
-
-        wq = {}
-        ws = {}
+        def x_quantise(operand):
+            key = divmod(operand, D_PASSES)
+            x_codes[key] = keep.tile([P, PASS], U32, name="x_codes%d" % operand, align_bytes=256)
+            x_scales[key] = keep.tile([P, PASS], U8, name="x_scales%d" % operand, align_bytes=256)
+            nc.vector.quantize_mx(out=x_codes[key][:].bitcast(FP8X4), scales=x_scales[key][:], in_=x_grouped[key][:])
 
         w_grouped = {}
+        w_codes = {}
+        w_scales = {}
 
-        def w_interleave_gpsimd(j, dst):
-            w_grouped[j] = dst
-            src = w_raw[divmod(j, KP)][:].rearrange("p t m -> p m t")
+        def w_tile(piece):
+            own = keep.tile([P, 4 * W_COLS], BF16, name="w_grouped%d" % piece, align_bytes=256)
+            return own[:]
+
+        def w_interleave_gpsimd(piece, dst):
+            w_grouped[piece] = dst
+            src = w_raw[piece][:].rearrange("p t m -> p m t")
             nc.gpsimd.tensor_scalar(
                 out=dst.rearrange("p (m t) -> p m t", t=4), in0=src, scalar1=1.0, scalar2=0.0, op0=ALU.mult, op1=ALU.add
             )
 
-        def w_own_tile(j):
-            own = keep.tile([P, 1024], BF16, name="w_grouped%d" % j, align_bytes=256)
-            return own[:]
-
-        def w_interleave_scalar(j, half):
+        def w_interleave_scalar(piece, half):
             if half == 0:
-                w_grouped[j] = w_own_tile(j)
-            src = w_raw[divmod(j, KP)][:, :, P * half : P * (half + 1)].rearrange("p t m -> p m t")
-            dst = w_grouped[j][:, PASS * half : PASS * (half + 1)]
+                w_grouped[piece] = w_tile(piece)
+            src = w_raw[piece][:, :, P * half : P * (half + 1)].rearrange("p t m -> p m t")
+            dst = w_grouped[piece][:, 4 * P * half : 4 * P * (half + 1)]
             nc.scalar.copy(out=dst.rearrange("p (m t) -> p m t", t=4), in_=src)
 
-        def w_quant(j):
-            q, kp = divmod(j, KP)
-            wq[q, kp] = keep.tile([P, 256], U32, name="wq%d" % j, align_bytes=256)
-            ws[q, kp] = keep.tile([P, 256], U8, name="ws%d" % j, align_bytes=256)
-            nc.vector.quantize_mx(out=wq[q, kp][:].bitcast(FP8X4), scales=ws[q, kp][:], in_=w_grouped[j])
+        def w_quantise(piece):
+            w_codes[piece] = keep.tile([P, W_COLS], U32, name="w_codes%d" % piece, align_bytes=256)
+            w_scales[piece] = keep.tile([P, W_COLS], U8, name="w_scales%d" % piece, align_bytes=256)
+            nc.vector.quantize_mx(out=w_codes[piece][:].bitcast(FP8X4), scales=w_scales[piece][:], in_=w_grouped[piece])
 
         ck = keep.tile([P, 2 * CHUNKS], F32, name="ck", align_bytes=64)
 
         def make_ck():
-            cb = bank(7, BF16)
-            nc.tensor.transpose(cb[:, 0:P], ck_rows[:], ident_bf[:])
-            nc.scalar.copy(out=ck[:], in_=cb[:, 0 : 2 * CHUNKS])
+            turned_ck = bank(SETUP_BANK, BF16)
+            nc.tensor.transpose(turned_ck[:, 0:P], ck_rows[:], ident_bf[:])
+            nc.scalar.copy(out=ck[:], in_=turned_ck[:, 0 : 2 * CHUNKS])
 
-        ab_rows = [keep.tile([P, N], BF16, name="a_rows", align_bytes=256), keep.tile([P, N], BF16, name="b_rows", align_bytes=256)]
+        def c_col(i):
+            return ck[:, i : i + 1]
 
-        def make_ab(j):
-            half, which = divmod(j, 2)
-            sb = bank((0, 1, 7, 7)[j], BF16)
+        def k_col(i):
+            return ck[:, CHUNKS + i : CHUNKS + i + 1]
+
+        a_rows = keep.tile([P, N], BF16, name="a_rows", align_bytes=256)
+        b_rows = keep.tile([P, N], BF16, name="b_rows", align_bytes=256)
+
+        def spread_ab(vector, half, index):
+            spread = bank(index, BF16)
             for at in range(2):
                 g = 2 * half + at
                 nc.tensor.matmul(
-                    out=sb[:, PASS * at : PASS * (at + 1)].rearrange("m (u p e) -> m u p e", u=2, e=2),
-                    lhsT=ident_bf[:, which : which + 1].to_broadcast([P, P]),
-                    rhs=ab_first[:, PASS * g : PASS * (g + 1)].rearrange("r (p u e) -> r u p e", u=2, e=2),
+                    out=spread[:, PASS * at : PASS * (at + 1)].rearrange("m (u p e) -> m u p e", u=2, e=2),
+                    lhsT=ident_bf[:, vector : vector + 1].to_broadcast([P, P]),
+                    rhs=ab_loaded[:, PASS * g : PASS * (g + 1)].rearrange("r (p u e) -> r u p e", u=2, e=2),
                     start=True,
                     stop=True,
                 )
-            nc.scalar.copy(out=ab_rows[which][:, 2 * PASS * half : 2 * PASS * (half + 1)], in_=sb[:])
+            nc.scalar.copy(out=(a_rows, b_rows)[vector][:, 2 * PASS * half : 2 * PASS * (half + 1)], in_=spread[:])
 
         units = [(s, g, i) for s, chunks in enumerate(STEPS) for g in range(GROUPS) for i in chunks]
-        n_units = len(units)
+        last_chunk = len(units) - GROUPS
         y_bank = {}
         y_index = {}
-        th = {}
-        fh_t = {}
-        quantised = [[0, 0] for s in STEPS]
-        fh_grouped = {}
-        fq = [keep.tile([P, M], U32, name="fq%d" % g, align_bytes=256) for g in range(GROUPS)]
-        fs = [keep.tile([P, M], U8, name="fs%d" % g, align_bytes=256) for g in range(GROUPS)]
-        hq = [keep.tile([P, M], U32, name="hq%d" % g, align_bytes=256) for g in range(GROUPS)]
-        hs = [keep.tile([P, M], U8, name="hs%d" % g, align_bytes=256) for g in range(GROUPS)]
-
-        fh_codes = (hq, fq)
-        fh_scales = (hs, fs)
+        tanh_y = {}
         affine = {}
+        f_sum = {}
+        fh_rounded = {}
+        turned = {}
+        fh_grouped = {}
+        f_codes = [keep.tile([P, M], U32, name="f_codes%d" % g, align_bytes=256) for g in range(GROUPS)]
+        f_scales = [keep.tile([P, M], U8, name="f_scales%d" % g, align_bytes=256) for g in range(GROUPS)]
+        h_codes = [keep.tile([P, M], U32, name="h_codes%d" % g, align_bytes=256) for g in range(GROUPS)]
+        h_scales = [keep.tile([P, M], U8, name="h_scales%d" % g, align_bytes=256) for g in range(GROUPS)]
+        groups_quantised = [[0, 0] for s in STEPS]
 
         def on_gpsimd(n):
-            return n < MIXED or ((n - MIXED) % 2 == 0 and n + 1 < SHARED_UNITS)
+            return n < MIXED or (n < last_chunk and (n - MIXED) % 2 == 0)
 
         def y_matmul(n):
             s, g, i = units[n]
-            q, half = divmod(i, 2)
-            y_index[n] = rotate(y_banks)
+            quarter, half = divmod(i, 2)
+            cols = slice(P * half, P * (half + 1))
+            y_index[n] = rotate(unit_banks)
             y_bank[n] = bank(y_index[n])
-            for kp in range(KP):
-                cols = slice(P * half, P * (half + 1))
+            for dp in range(D_PASSES):
+                piece = D_PASSES * quarter + dp
                 nc.tensor.matmul_mx(
                     out=y_bank[n][:],
-                    lhsT=wq[q, kp][:, cols].bitcast(FP8X4),
-                    lhsT_scale=ws[q, kp][:, cols],
-                    rhs=xq[g, kp][:].bitcast(FP8X4),
-                    rhs_scale=xs[g, kp][:],
-                    start=(kp == 0),
-                    stop=(kp == KP - 1),
+                    lhsT=w_codes[piece][:, cols].bitcast(FP8X4),
+                    lhsT_scale=w_scales[piece][:, cols],
+                    rhs=x_codes[g, dp][:].bitcast(FP8X4),
+                    rhs_scale=x_scales[g, dp][:],
+                    start=(dp == 0),
+                    stop=(dp == D_PASSES - 1),
                 )
 
         def y_tanh(n):
             s, g, i = units[n]
-            th[n] = work.tile([P, PASS], F32, name="th", bufs=5, align_bytes=256)
-            nc.scalar.activation(out=th[n][:], in_=y_bank[n][:], func=ACT.Tanh, bias=ck[:, i : i + 1], scale=1.0)
+            tanh_y[n] = work.tile([P, PASS], F32, name="tanh_y", bufs=5, align_bytes=256)
+            nc.scalar.activation(out=tanh_y[n][:], in_=y_bank[n][:], func=ACT.Tanh, bias=c_col(i), scale=1.0)
 
         def y_affine(n):
             s, g, i = units[n]
             if on_gpsimd(n):
                 affine[n] = work.tile([P, PASS], F32, name="affine", bufs=3, align_bytes=256)
-                nc.scalar.activation(
-                    out=affine[n][:], in_=th[n][:], func=ACT.Identity, bias=ck[:, i : i + 1], scale=ck[:, CHUNKS + i : CHUNKS + i + 1]
-                )
+                nc.scalar.activation(out=affine[n][:], in_=tanh_y[n][:], func=ACT.Identity, bias=c_col(i), scale=k_col(i))
 
-        part = {}
-
-        def f_sum(n):
+        def make_f_sum(n):
             s, g, i = units[n]
-            part[n] = work.tile([P, PASS], F32, name="part", bufs=2, align_bytes=256)
+            f_sum[n] = work.tile([P, PASS], F32, name="f_sum", bufs=2, align_bytes=256)
             if on_gpsimd(n):
-                nc.vector.tensor_tensor(out=part[n][:], in0=affine[n][:], in1=y_bank[n][:], op=ALU.add)
+                nc.vector.tensor_tensor(out=f_sum[n][:], in0=affine[n][:], in1=y_bank[n][:], op=ALU.add)
             else:
                 nc.vector.scalar_tensor_tensor(
-                    out=part[n][:], in0=th[n][:], scalar=ck[:, CHUNKS + i : CHUNKS + i + 1], in1=y_bank[n][:], op0=ALU.mult, op1=ALU.add
+                    out=f_sum[n][:], in0=tanh_y[n][:], scalar=k_col(i), in1=y_bank[n][:], op0=ALU.mult, op1=ALU.add
                 )
 
         def make_f(n):
             s, g, i = units[n]
-            a_row = ab_rows[0][:, PASS * g : PASS * (g + 1)]
-            fh_t[n, F] = work.tile([P, PASS], BF16, name="f_t", bufs=3, align_bytes=256)
+            a_row = a_rows[:, PASS * g : PASS * (g + 1)]
+            fh_rounded[n, F] = work.tile([P, PASS], BF16, name="f_rounded", bufs=3, align_bytes=256)
             if on_gpsimd(n):
-                nc.gpsimd.tensor_tensor(out=fh_t[n, F][:], in0=part[n][:], in1=a_row, op=ALU.mult)
+                nc.gpsimd.tensor_tensor(out=fh_rounded[n, F][:], in0=f_sum[n][:], in1=a_row, op=ALU.mult)
             else:
                 nc.vector.scalar_tensor_tensor(
-                    out=fh_t[n, F][:], in0=part[n][:], scalar=ck[:, i : i + 1], in1=a_row, op0=ALU.add, op1=ALU.mult
+                    out=fh_rounded[n, F][:], in0=f_sum[n][:], scalar=c_col(i), in1=a_row, op0=ALU.add, op1=ALU.mult
                 )
 
         def make_h(n):
             s, g, i = units[n]
-            b_row = ab_rows[1][:, PASS * g : PASS * (g + 1)]
-            fh_t[n, H] = work.tile([P, PASS], BF16, name="h_t", bufs=3, align_bytes=256)
+            b_row = b_rows[:, PASS * g : PASS * (g + 1)]
+            fh_rounded[n, H] = work.tile([P, PASS], BF16, name="h_rounded", bufs=3, align_bytes=256)
             nc.vector.scalar_tensor_tensor(
-                out=fh_t[n, H][:], in0=y_bank[n][:], scalar=ck[:, i : i + 1], in1=b_row, op0=ALU.add, op1=ALU.mult
+                out=fh_rounded[n, H][:], in0=y_bank[n][:], scalar=c_col(i), in1=b_row, op0=ALU.add, op1=ALU.mult
             )
 
         def elementwise(n):
-            f_sum(n)
+            make_f_sum(n)
             if on_gpsimd(n):
                 make_f(n)
                 make_h(n)
@@ -299,279 +295,285 @@ def tile_extendedinfomaxicarelativegrad_kernel(tc, x_bytes, x_scale, w, c, k, a,
                 make_h(n)
                 make_f(n)
 
-        turned = {}
-
         def turn(items):
-            tb = turn_bank()
-            for at, item in enumerate(items):
-                words = fh_t[item][:].bitcast(F32)
-                turned[item] = (tb, at)
+            turned_fh = bank(rotate(turn_banks))
+            for half, item in enumerate(items):
+                words = fh_rounded[item][:].bitcast(F32)
+                turned[item] = (turned_fh, half)
                 for u in range(2):
-                    s = 2 * at + u
-                    nc.tensor.transpose(tb[:, s * P : (s + 1) * P], words[:, u * P : (u + 1) * P], ident[:])
+                    at = P * (2 * half + u)
+                    nc.tensor.transpose(turned_fh[:, at : at + P], words[:, u * P : (u + 1) * P], ident[:])
 
         def regroup(n, which):
             s, g, i = units[n]
-            width = len(STEPS[s])
-            place = STEPS[s].index(i)
+            n_chunks = len(STEPS[s])
             if (s, g) not in fh_grouped:
-                fh_grouped[s, g] = work.tile([P, 2 * width * PASS], BF16, name="fh_grouped", bufs=3, align_bytes=256)
-            words = fh_grouped[s, g][:].bitcast(F32).rearrange("p (j i m u) -> p j i m u", j=2, i=width, u=2)
-            tb, at = turned[n, which[0]]
-            src = tb[:].rearrange("p (j u m) -> p j m u", j=2, u=2)
-            nc.scalar.copy(out=words[:, which[0] : which[-1] + 1, place, :, :], in_=src[:, at : at + len(which), :, :])
+                fh_grouped[s, g] = work.tile([P, 2 * n_chunks * PASS], BF16, name="fh_grouped", bufs=3, align_bytes=256)
+            words = fh_grouped[s, g][:].bitcast(F32).rearrange("p (j i m u) -> p j i m u", j=2, i=n_chunks, u=2)
+            turned_fh, half = turned[n, which[0]]
+            src = turned_fh[:].rearrange("p (j u m) -> p j m u", j=2, u=2)
+            nc.scalar.copy(out=words[:, which[0] : which[-1] + 1, STEPS[s].index(i), :, :], in_=src[:, half : half + len(which), :, :])
 
-        def fh_quant(n, which):
+        def fh_quantise(n, which):
             s, g, i = units[n]
             if i != STEPS[s][-1]:
                 return
-            width = len(STEPS[s])
+            values = len(STEPS[s]) * PASS
             cols = slice(P * STEPS[s][0], P * (i + 1))
-            for j in which:
+            for side in which:
                 nc.vector.quantize_mx(
-                    out=fh_codes[j][g][:, cols].bitcast(FP8X4),
-                    scales=fh_scales[j][g][:, cols],
-                    in_=fh_grouped[s, g][:, j * width * PASS : (j + 1) * width * PASS],
+                    out=(h_codes, f_codes)[side][g][:, cols].bitcast(FP8X4),
+                    scales=(h_scales, f_scales)[side][g][:, cols],
+                    in_=fh_grouped[s, g][:, side * values : (side + 1) * values],
                 )
-                quantised[s][j] = g + 1
+                groups_quantised[s][side] = g + 1
 
-        def sums_of(job):
+        jobs = [job for step_jobs in JOBS for job in step_jobs]
+        job_step = [s for s, step_jobs in enumerate(JOBS) for job in step_jobs]
+        job_bank = []
+        job_index = []
+        passes_done = [0] * len(jobs)
+        results = []
+        stored = []
+
+        def sums_of(j):
             sums = []
             place = 0
-            for row0, rows, col0, width in job:
-                for r in range(rows):
-                    sums.append((row0 + r, col0, width, place))
+            for row0, rows, col0, width in jobs[j]:
+                for row in range(row0, row0 + rows):
+                    sums.append((row, col0, width, place))
                     place = place + width
             return sums
 
-        def m_pass(acc, one_sum, g, start, stop):
-            row, col0, width, place = one_sum
-            rows = slice(P * row, P * (row + 1))
-            cols = slice(col0, col0 + width)
-            nc.tensor.matmul_mx(
-                out=acc[:, place : place + width],
-                lhsT=fq[g][:, rows].bitcast(FP8X4),
-                lhsT_scale=fs[g][:, rows],
-                rhs=hq[g][:, cols].bitcast(FP8X4),
-                rhs_scale=hs[g][:, cols],
-                start=start,
-                stop=stop,
-            )
+        def diagonal_places(j):
+            return [place + P * row - col0 for row, col0, width, place in sums_of(j) if col0 <= P * row < col0 + width]
 
-        def diagonal_places(job):
-            return [place + P * row - col0 for row, col0, width, place in sums_of(job) if col0 <= P * row < col0 + width]
+        def groups_ready(j):
+            s = job_step[j]
+            needs_f = any(row in STEPS[s] for row, col0, width, place in sums_of(j))
+            return min(groups_quantised[s]) if needs_f else groups_quantised[s][H]
 
-        def finish(job, acc):
-            result = work.tile([P, 512], F32, name="result", bufs=6, align_bytes=256)
-            nc.scalar.activation(out=result[:], in_=acc[:], func=ACT.Copy, scale=-1.0 / ROOT_N)
+        def job_passes(limit=len(jobs)):
+            while len(job_bank) < limit and free_job_banks and groups_ready(len(job_bank)) > 0:
+                index = free_job_banks[0]
+                free_job_banks.remove(index)
+                job_bank.append(bank(index))
+                job_index.append(index)
+            for j in range(len(results), min(limit, len(job_bank))):
+                sums = sums_of(j)
+                for g in range(passes_done[j], groups_ready(j)):
+                    for at, (row, col0, width, place) in enumerate(sums):
+                        f_cols = slice(P * row, P * (row + 1))
+                        h_cols = slice(col0, col0 + width)
+                        nc.tensor.matmul_mx(
+                            out=job_bank[j][:, place : place + width],
+                            lhsT=f_codes[g][:, f_cols].bitcast(FP8X4),
+                            lhsT_scale=f_scales[g][:, f_cols],
+                            rhs=h_codes[g][:, h_cols].bitcast(FP8X4),
+                            rhs_scale=h_scales[g][:, h_cols],
+                            start=(g == 0 and at == 0),
+                            stop=(g == GROUPS - 1 and at == len(sums) - 1),
+                        )
+                passes_done[j] = groups_ready(j)
+
+        def result_tile():
+            return work.tile([P, PASS], F32, name="result", bufs=6, align_bytes=256)
+
+        def copy_out_scalar(j):
+            result = result_tile()
+            used = sum(width for row, col0, width, place in sums_of(j))
+            nc.scalar.activation(out=result[:, 0:used], in_=job_bank[j][:, 0:used], func=ACT.Copy, scale=-1.0 / ROOT_N)
             return result
 
-        def finish_on_vector(job, acc):
-            result = work.tile([P, 512], F32, name="result", bufs=6, align_bytes=256)
-            (at,) = diagonal_places(job)
-            nc.vector.tensor_scalar(out=result[:, 0:at], in0=acc[:, 0:at], scalar1=-1.0 / ROOT_N, scalar2=None, op0=ALU.mult)
+        def copy_out_vector(j):
+            result = result_tile()
+            (at,) = diagonal_places(j)
+            plain = slice(P, PASS) if at == 0 else slice(0, at)
+            block = slice(at, at + P)
+            nc.vector.tensor_scalar(out=result[:, plain], in0=job_bank[j][:, plain], scalar1=-1.0 / ROOT_N, scalar2=None, op0=ALU.mult)
             nc.vector.scalar_tensor_tensor(
-                out=result[:, at:], in0=acc[:, at:], scalar=-1.0 / ROOT_N, in1=root_ident[:], op0=ALU.mult, op1=ALU.add
+                out=result[:, block], in0=job_bank[j][:, block], scalar=-1.0 / ROOT_N, in1=root_ident[:], op0=ALU.mult, op1=ALU.add
             )
             return result
 
-        def add_diagonal(job, result):
-            for at in diagonal_places(job):
-                nc.vector.tensor_tensor(out=result[:, at : at + P], in0=result[:, at : at + P], in1=root_ident[:], op=ALU.add)
-
-        def store(job, result):
+        def store(j, result):
             place = 0
-            for row0, rows, col0, width in job:
+            for row0, rows, col0, width in jobs[j]:
                 nc.sync.dma_start(
                     out=out[P * row0 : P * (row0 + rows), col0 : col0 + width].rearrange("(r p) m -> p r m", p=P),
                     in_=result[:, place : place + rows * width].rearrange("p (r m) -> p r m", r=rows),
                 )
                 place = place + rows * width
 
-        jobs = [(s, job) for s in range(len(STEPS)) for job in JOBS[s]]
-        free_banks = [7]
-        accs = []
-        passes_done = [0] * len(jobs)
-        results = []
-
-        def groups_ready(j):
-            s, job = jobs[j]
-            new_rows = any(row in STEPS[s] for row, col0, width, place in sums_of(job))
-            return min(quantised[s]) if new_rows else quantised[s][H]
-
-        def open_jobs_and_pass(limit=len(jobs)):
-            while len(accs) < limit and free_banks and groups_ready(len(accs)) > 0:
-                index = free_banks[0]
-                free_banks.remove(index)
-                accs.append((bank(index), index))
-            for j in range(len(results), min(limit, len(accs))):
-                sums = sums_of(jobs[j][1])
-                for g in range(passes_done[j], groups_ready(j)):
-                    for at, one_sum in enumerate(sums):
-                        m_pass(accs[j][0], one_sum, g, g == 0 and at == 0, g == GROUPS - 1 and at == len(sums) - 1)
-                passes_done[j] = groups_ready(j)
-
         def finish_next():
             j = len(results)
             if passes_done[j] == GROUPS:
-                results.append(finish(jobs[j][1], accs[j][0]))
-                free_banks.append(accs[j][1])
-
-        stored = []
+                results.append(copy_out_scalar(j))
+                free_job_banks.append(job_index[j])
 
         def store_up_to(count):
             for j in range(len(stored), count):
-                add_diagonal(jobs[j][1], results[j])
-                store(jobs[j][1], results[j])
+                for at in diagonal_places(j):
+                    block = results[j][:, at : at + P]
+                    nc.vector.tensor_tensor(out=block, in0=block, in1=root_ident[:], op=ALU.add)
+                store(j, results[j])
                 stored.append(j)
 
-        for j in range(3):
-            w_interleave_gpsimd(j, w_own_tile(j))
-        for h in range(X_ALONE):
-            x_scale_unit(h)
-            if h >= 6:
-                y_affine(h - 6)
-            if h in (4, 5):
-                w_interleave_scalar(W_ON_GPSIMD, h - 4)
-            x_turn(h)
-            if h == 1:
+        for piece in range(W_ON_GPSIMD - 1):
+            w_interleave_gpsimd(piece, w_tile(piece))
+        for part in range(X_ALONE):
+            x_widen(part)
+            if part >= 6:
+                y_affine(part - 6)
+            if part in (4, 5):
+                w_interleave_scalar(W_ON_GPSIMD, part - 4)
+            x_turn(part)
+            if part == 1:
                 make_ck()
-            if h in AB_AT:
-                make_ab(AB_AT.index(h))
-            if h == 4:
-                for j in range(3):
-                    w_quant(j)
-                x_quant(0)
-            if h == 5:
-                x_quant(1)
-                w_interleave_gpsimd(3, x_grouped[0, 1][:, 0:1024])
-            if h in (5, 6):
-                y_matmul(h - 5)
-                y_tanh(h - 5)
-            if h == 7:
-                w_quant(3)
-                x_quant(2)
+            if part < 2:
+                spread_ab(part, 0, unit_banks[part])
+            if part in (AB_SECOND_HALF, AB_SECOND_HALF + 1):
+                spread_ab(part - AB_SECOND_HALF, 1, SETUP_BANK)
+            if part == 4:
+                for piece in range(W_ON_GPSIMD - 1):
+                    w_quantise(piece)
+                x_quantise(0)
+            if part == 5:
+                x_quantise(1)
+                w_interleave_gpsimd(W_ON_GPSIMD - 1, x_grouped[0, 1][:, 0 : 4 * W_COLS])
+            if part in (5, 6):
+                y_matmul(part - 5)
+                y_tanh(part - 5)
+            if part == 7:
+                w_quantise(W_ON_GPSIMD - 1)
+                x_quantise(2)
 
-        x_done = KP + 1
         for n in range(MIXED):
-            h = X_ALONE + n
+            part = X_ALONE + n
             elementwise(n)
             y_matmul(n + 2)
             y_tanh(n + 2)
-            if n < 6:
-                w_interleave_scalar(W_ON_GPSIMD + 1 + n // 2, n % 2)
+            if n < 2:
+                w_interleave_scalar(W_ON_GPSIMD + 1, n)
             y_affine(n + 2)
-            x_scale_unit(h)
-            if 2 * x_done + 2 < h:
-                x_quant(x_done)
-                x_done = x_done + 1
+            x_widen(part)
+            if part % 2 == 1:
+                x_quantise((part - 3) // 2)
             if n >= 2:
-                fh_quant(n - 2, BOTH)
+                fh_quantise(n - 2, BOTH)
             if n in (3, 5):
-                w_quant(W_ON_GPSIMD + (n - 3) // 2)
+                w_quantise(W_ON_GPSIMD + (n - 3) // 2)
             turn([(n, H), (n, F)])
             regroup(n, BOTH)
-            x_turn(h)
-            open_jobs_and_pass()
-        n_quantised = MIXED - 2
-        turn_banks.remove(2)
-        y_banks.remove(y_index[MIXED])
-        y_banks.remove(y_index[MIXED + 1])
-        y_banks.extend([2, y_index[MIXED], y_index[MIXED + 1]])
-        free_banks.extend([5, 6])
+            x_turn(part)
+            job_passes()
+
+        turn_banks.remove(THIRD_UNIT_BANK)
+        unit_banks.clear()
+        unit_banks.extend([THIRD_UNIT_BANK, y_index[MIXED], y_index[MIXED + 1]])
+        free_job_banks.extend(SCALE_BANKS)
         y_matmul(MIXED + 2)
         y_tanh(MIXED + 2)
         y_affine(MIXED + 2)
 
-        last = n_units - GROUPS
-        n = MIXED
-        while n < last:
-            batch = [n, n + 1] if on_gpsimd(n) else [n]
-            finished_earlier = len(results)
-            open_jobs_and_pass()
-            for m in batch:
+        last_pieces = (2 * D_PASSES + 2, 2 * D_PASSES + 3)
+        first_of_chunk_6 = last_chunk - GROUPS
+        not_quantised = MIXED - 2
+        for n in range(MIXED, last_chunk, 2):
+            pair = (n, n + 1)
+            copied_out = len(results)
+            job_passes()
+            for m in pair:
                 elementwise(m)
-                if (units[m + 3][1], KP - 1) in xq:
+                if (units[m + 3][1], D_PASSES - 1) in x_codes:
                     y_matmul(m + 3)
                     finish_next()
                     y_tanh(m + 3)
-            for m in batch:
+            for m in pair:
                 turn([(m, H), (m, F)])
-            store_up_to(finished_earlier)
-            for m in range(n_quantised, n):
-                fh_quant(m, BOTH)
-            n_quantised = n
-            if n == 18:
-                w_quant(6)
-                w_quant(7)
+            store_up_to(copied_out)
+            for m in range(not_quantised, n):
+                fh_quantise(m, BOTH)
+            not_quantised = n
+            if n + 6 == first_of_chunk_6:
+                for piece in last_pieces:
+                    w_quantise(piece)
             if n == MIXED:
-                x_quant(GROUPS * KP - 1)
+                x_quantise(GROUPS * D_PASSES - 1)
                 y_matmul(n + 4)
-            for m in batch:
+            for m in pair:
                 regroup(m, BOTH)
             if n == MIXED:
                 y_tanh(n + 4)
-            for m in batch:
+            for m in pair:
                 y_affine(m + 3)
-            n = n + len(batch)
+            if n < MIXED + 8:
+                dp, half = divmod((n - MIXED) // 2, 2)
+                w_interleave_scalar(last_pieces[dp], half)
 
-        u0, u1, u2, u3 = range(last, n_units)
-        strips = len(jobs) - 2
-        open_jobs_and_pass()
-        f_sum(u0)
-        make_h(u0)
-        y_matmul(u3)
+        n0, n1, n2, n3 = range(last_chunk, len(units))
+        first_of_step = len(jobs) - len(JOBS[-1])
+        first_of_row_7 = len(jobs) - 3
+        job_passes()
+        make_f_sum(n0)
+        make_h(n0)
+        y_matmul(n3)
         finish_next()
-        y_tanh(u3)
-        make_h(u1)
-        make_f(u0)
-        turn([(u0, H), (u0, F)])
-        regroup(u0, BOTH)
-        open_jobs_and_pass()
-        for m in range(n_quantised, u0):
-            fh_quant(m, BOTH)
-        open_jobs_and_pass(strips - 3)
+        y_tanh(n3)
+        make_h(n1)
+        make_f(n0)
+        turn([(n0, H), (n0, F)])
+        regroup(n0, BOTH)
+        job_passes()
+        for m in range(not_quantised, n0):
+            fh_quantise(m, BOTH)
+        job_passes(first_of_step - 1)
         finish_next()
-        f_sum(u1)
-        free_banks.append(y_index[u1])
-        make_h(u2)
+
+        make_f_sum(n1)
+        free_job_banks.append(y_index[n1])
+        make_h(n2)
         store_up_to(len(results))
-        turn([(u1, H), (u2, H)])
-        regroup(u1, (H,))
-        regroup(u2, (H,))
-        open_jobs_and_pass(strips - 2)
+        turn([(n1, H), (n2, H)])
+        regroup(n1, (H,))
+        regroup(n2, (H,))
+        job_passes(first_of_step)
         finish_next()
-        make_f(u1)
-        make_h(u3)
-        fh_quant(u0, BOTH)
-        turn([(u1, F), (u3, H)])
-        regroup(u3, (H,))
-        regroup(u1, (F,))
+        make_f(n1)
+        make_h(n3)
+        fh_quantise(n0, BOTH)
+        turn([(n1, F), (n3, H)])
+        regroup(n3, (H,))
+        regroup(n1, (F,))
         finish_next()
         store_up_to(len(results))
-        open_jobs_and_pass(strips)
-        f_sum(u2)
-        fh_quant(u1, (H,))
-        fh_quant(u2, (H,))
-        open_jobs_and_pass(strips - 1)
-        make_f(u2)
-        turn([(u2, F)])
-        regroup(u2, (F,))
-        open_jobs_and_pass(strips)
-        f_sum(u3)
-        fh_quant(u3, (H,))
-        fh_quant(u1, (F,))
-        open_jobs_and_pass(strips - 1)
-        make_f(u3)
-        turn([(u3, F)])
-        regroup(u3, (F,))
+        job_passes(first_of_row_7)
+
+        make_f_sum(n2)
+        fh_quantise(n1, (H,))
+        fh_quantise(n2, (H,))
+        job_passes(first_of_step + 1)
+        make_f(n2)
+        turn([(n2, F)])
+        regroup(n2, (F,))
+        job_passes(first_of_row_7)
+        free_job_banks.append(y_index[n2])
+
+        make_f_sum(n3)
+        fh_quantise(n3, (H,))
+        fh_quantise(n1, (F,))
+        job_passes(first_of_step + 1)
+        make_f(n3)
+        turn([(n3, F)])
+        regroup(n3, (F,))
         finish_next()
-        open_jobs_and_pass(strips)
-        finish_next()
-        fh_quant(u2, (F,))
-        open_jobs_and_pass()
-        fh_quant(u3, (F,))
-        open_jobs_and_pass()
+        job_passes(first_of_row_7)
+        fh_quantise(n2, (F,))
+        job_passes(first_of_row_7 + 1)
+        fh_quantise(n3, (F,))
+        job_passes()
         store_up_to(len(results))
-        store(jobs[strips][1], finish_on_vector(jobs[strips][1], accs[strips][0]))
-        store(jobs[strips + 1][1], finish(jobs[strips + 1][1], accs[strips + 1][0]))
+        for j in (first_of_row_7 - 1, first_of_row_7):
+            store(j, copy_out_vector(j))
+        for j in (first_of_row_7 + 1, first_of_row_7 + 2):
+            store(j, copy_out_scalar(j))

import math
from contextlib import ExitStack

import concourse.mybir as mybir
from concourse.masks import make_identity

N, D, M = 2048, 1024, 1024
FLOPS = 2 * N * D * M + 2 * N * M * M

F32 = mybir.dt.float32
BF16 = mybir.dt.bfloat16
U32 = mybir.dt.uint32
I32 = mybir.dt.int32
U8 = mybir.dt.uint8
FP8 = mybir.dt.float8_e4m3fn
FP8X4 = mybir.dt.float8_e4m3fn_x4
ALU = mybir.AluOpType
ACT = mybir.ActivationFunctionType

P = 128
PASS = 512
GROUPS = N // PASS
D_PASSES = D // PASS
CHUNKS = M // P
W_COLS = 256
ROOT_N = math.sqrt(N)
H, F = 0, 1
BOTH = (H, F)

X_PARTS = GROUPS * D_PASSES * 2
X_ALONE = 8
MIXED = X_PARTS - X_ALONE
W_ON_GPSIMD = 4
AB_SECOND_HALF = 3

STEPS = [(0, 1, 2, 3), (4,), (5,), (6,), (7,)]
JOBS = [
    [[(0, 1, 0, 512)], [(1, 1, 0, 512)], [(2, 1, 0, 512)], [(3, 1, 0, 512)]],
    [[(4, 1, 0, 512)], [(0, 4, 512, 128)]],
    [[(5, 1, 0, 512)], [(0, 4, 640, 128)], [(4, 2, 512, 256)]],
    [[(6, 1, 0, 512)], [(0, 4, 768, 128)], [(6, 1, 512, 256), (4, 2, 768, 128)]],
    [[(0, 4, 896, 128)], [(6, 1, 768, 256), (4, 2, 896, 128)], [(7, 1, 512, 512)], [(7, 1, 0, 256)], [(7, 1, 256, 256)]],
]

SCALE_BANKS = (5, 6)
SETUP_BANK = 7
THIRD_UNIT_BANK = 2


def tile_extendedinfomaxicarelativegrad_kernel(tc, x_bytes, x_scale, w, c, k, a, b, out):
    nc = tc.nc
    with ExitStack() as ctx:
        keep = ctx.enter_context(tc.tile_pool(name="keep", bufs=1))
        work = ctx.enter_context(tc.tile_pool(name="work", bufs=3))
        psum = ctx.enter_context(tc.psum_pool(name="psum", bufs=1))
        ctx.enter_context(tc.manual_schedule())

        def bank(index, dtype=F32):
            return psum.tile([P, PASS if dtype == F32 else 2 * PASS], dtype, name="bank%d" % index, tag="bank%d" % index)

        turn_banks = [THIRD_UNIT_BANK, 3, 4]
        unit_banks = [0, 1]
        free_job_banks = [SETUP_BANK]

        def rotate(indices):
            index = indices[0]
            indices.remove(index)
            indices.append(index)
            return index

        ident = keep.tile([P, P], F32, name="ident", align_bytes=64)
        make_identity(nc, ident[:])
        ck_rows = keep.tile([P, P], BF16, name="ck_rows", align_bytes=64)
        nc.gpsimd.memset(ck_rows[:], 0.0)
        ident_bf = keep.tile([P, P], BF16, name="ident_bf", align_bytes=64)
        make_identity(nc, ident_bf[:])
        root_ident = keep.tile([P, P], F32, name="root_ident", align_bytes=64)
        nc.gpsimd.tensor_scalar(out=root_ident[:], in0=ident[:], scalar1=ROOT_N, scalar2=0.0, op0=ALU.mult, op1=ALU.add)
        ab_loaded = keep.tile([P, N], BF16, name="ab_loaded", align_bytes=256)
        nc.vector.memset(ab_loaded[:].bitcast(I32), 0)

        scale_cols = keep.tile([P, D_PASSES, 4], F32, name="scale_cols", align_bytes=64)
        nc.sync.dma_start(out=scale_cols[:], in_=x_scale.rearrange("o (g p t) -> p (o g) t", p=P, t=4))

        x_view = x_bytes.rearrange("(g q j) d -> g q j d", q=P, j=4)
        w_view = w.rearrange("(g p t) m -> g p t m", p=P, t=4)
        x_raw = {}
        w_raw = {}

        def load_x(g):
            for u in range(2):
                x_raw[g, u] = keep.tile([P, 2, D], U8, name="xbytes%d%d" % (g, u), align_bytes=256)
                nc.sync.dma_start(out=x_raw[g, u][:], in_=x_view[g, :, 2 * u : 2 * u + 2, :])

        def load_w(quarter):
            for dp in range(D_PASSES):
                piece = D_PASSES * quarter + dp
                w_raw[piece] = keep.tile([P, 4, W_COLS], BF16, name="wraw%d" % piece, align_bytes=256)
                nc.sync.dma_start(out=w_raw[piece][:], in_=w_view[dp, :, :, W_COLS * quarter : W_COLS * (quarter + 1)])

        load_x(0)
        load_w(0)
        nc.sync.dma_start(out=ck_rows[0:CHUNKS, :], in_=c.rearrange("(i p) -> i p", p=P))
        nc.sync.dma_start(out=ck_rows[CHUNKS : 2 * CHUNKS, :], in_=k.rearrange("(i p) -> i p", p=P))
        nc.sync.dma_start(out=ab_loaded[0:1, :], in_=a.rearrange("(o n) -> o n", o=1))
        nc.sync.dma_start(out=ab_loaded[1:2, :], in_=b.rearrange("(o n) -> o n", o=1))
        load_w(1)
        load_x(1)
        load_w(2)
        load_x(2)
        load_x(3)
        load_w(3)

        scale_rows = []
        for dp in range(D_PASSES):
            scale_rows.append(bank(SCALE_BANKS[dp]))
            for t in range(4):
                nc.tensor.transpose(scale_rows[dp][:, t:PASS:4], scale_cols[:, dp, t : t + 1].to_broadcast([P, P]), ident[:])

        x_parts = [(g, dp, u) for g in range(GROUPS) for dp in range(D_PASSES) for u in range(2)]
        x_scaled = {}
        x_grouped = {}
        x_codes = {}
        x_scales = {}

        def x_widen(part):
            g, dp, u = x_parts[part]
            x_scaled[part] = work.tile([P, 2, PASS], BF16, name="x_scaled", bufs=4, align_bytes=256)
            for e in range(2):
                nc.vector.tensor_tensor(
                    out=x_scaled[part][:, e, :],
                    in0=x_raw[g, u][:, e, dp * PASS : (dp + 1) * PASS].bitcast(FP8),
                    in1=scale_rows[dp][:],
                    op=ALU.mult,
                )

        def x_turn(part):
            g, dp, u = x_parts[part]
            words = x_scaled[part][:].rearrange("p e d -> p (e d)").bitcast(F32)
            turned_x = bank(rotate(turn_banks))
            for e in range(2):
                for v in range(2):
                    at = P * (2 * e + v)
                    nc.tensor.transpose(turned_x[:, at : at + P], words[:, 256 * e + v : 256 * (e + 1) : 2], ident[:])
            if u == 0:
                x_grouped[g, dp] = work.tile([P, 4 * PASS], BF16, name="x_grouped", bufs=4, align_bytes=256)
            dst = x_grouped[g, dp][:].bitcast(F32)[:, PASS * u : PASS * (u + 1)]
            nc.scalar.copy(out=dst.rearrange("p (q s) -> p q s", s=4), in_=turned_x[:].rearrange("p (s q) -> p q s", s=4))

        def x_quantise(operand):
            key = divmod(operand, D_PASSES)
            x_codes[key] = keep.tile([P, PASS], U32, name="x_codes%d" % operand, align_bytes=256)
            x_scales[key] = keep.tile([P, PASS], U8, name="x_scales%d" % operand, align_bytes=256)
            nc.vector.quantize_mx(out=x_codes[key][:].bitcast(FP8X4), scales=x_scales[key][:], in_=x_grouped[key][:])

        w_grouped = {}
        w_codes = {}
        w_scales = {}

        def w_tile(piece):
            own = keep.tile([P, 4 * W_COLS], BF16, name="w_grouped%d" % piece, align_bytes=256)
            return own[:]

        def w_interleave_gpsimd(piece, dst):
            w_grouped[piece] = dst
            src = w_raw[piece][:].rearrange("p t m -> p m t")
            nc.gpsimd.tensor_scalar(
                out=dst.rearrange("p (m t) -> p m t", t=4), in0=src, scalar1=1.0, scalar2=0.0, op0=ALU.mult, op1=ALU.add
            )

        def w_interleave_scalar(piece, half):
            if half == 0:
                w_grouped[piece] = w_tile(piece)
            src = w_raw[piece][:, :, P * half : P * (half + 1)].rearrange("p t m -> p m t")
            dst = w_grouped[piece][:, 4 * P * half : 4 * P * (half + 1)]
            nc.scalar.copy(out=dst.rearrange("p (m t) -> p m t", t=4), in_=src)

        def w_quantise(piece):
            w_codes[piece] = keep.tile([P, W_COLS], U32, name="w_codes%d" % piece, align_bytes=256)
            w_scales[piece] = keep.tile([P, W_COLS], U8, name="w_scales%d" % piece, align_bytes=256)
            nc.vector.quantize_mx(out=w_codes[piece][:].bitcast(FP8X4), scales=w_scales[piece][:], in_=w_grouped[piece])

        ck = keep.tile([P, 2 * CHUNKS], F32, name="ck", align_bytes=64)

        def make_ck():
            turned_ck = bank(SETUP_BANK, BF16)
            nc.tensor.transpose(turned_ck[:, 0:P], ck_rows[:], ident_bf[:])
            nc.scalar.copy(out=ck[:], in_=turned_ck[:, 0 : 2 * CHUNKS])

        def c_col(i):
            return ck[:, i : i + 1]

        def k_col(i):
            return ck[:, CHUNKS + i : CHUNKS + i + 1]

        a_rows = keep.tile([P, N], BF16, name="a_rows", align_bytes=256)
        b_rows = keep.tile([P, N], BF16, name="b_rows", align_bytes=256)

        def spread_ab(vector, half, index):
            spread = bank(index, BF16)
            for at in range(2):
                g = 2 * half + at
                nc.tensor.matmul(
                    out=spread[:, PASS * at : PASS * (at + 1)].rearrange("m (u p e) -> m u p e", u=2, e=2),
                    lhsT=ident_bf[:, vector : vector + 1].to_broadcast([P, P]),
                    rhs=ab_loaded[:, PASS * g : PASS * (g + 1)].rearrange("r (p u e) -> r u p e", u=2, e=2),
                    start=True,
                    stop=True,
                )
            nc.scalar.copy(out=(a_rows, b_rows)[vector][:, 2 * PASS * half : 2 * PASS * (half + 1)], in_=spread[:])

        units = [(s, g, i) for s, chunks in enumerate(STEPS) for g in range(GROUPS) for i in chunks]
        last_chunk = len(units) - GROUPS
        y_bank = {}
        y_index = {}
        tanh_y = {}
        affine = {}
        f_sum = {}
        fh_rounded = {}
        turned = {}
        fh_grouped = {}
        f_codes = [keep.tile([P, M], U32, name="f_codes%d" % g, align_bytes=256) for g in range(GROUPS)]
        f_scales = [keep.tile([P, M], U8, name="f_scales%d" % g, align_bytes=256) for g in range(GROUPS)]
        h_codes = [keep.tile([P, M], U32, name="h_codes%d" % g, align_bytes=256) for g in range(GROUPS)]
        h_scales = [keep.tile([P, M], U8, name="h_scales%d" % g, align_bytes=256) for g in range(GROUPS)]
        groups_quantised = [[0, 0] for s in STEPS]

        def on_gpsimd(n):
            return n < MIXED or (n < last_chunk and (n - MIXED) % 2 == 0)

        def y_matmul(n):
            s, g, i = units[n]
            quarter, half = divmod(i, 2)
            cols = slice(P * half, P * (half + 1))
            y_index[n] = rotate(unit_banks)
            y_bank[n] = bank(y_index[n])
            for dp in range(D_PASSES):
                piece = D_PASSES * quarter + dp
                nc.tensor.matmul_mx(
                    out=y_bank[n][:],
                    lhsT=w_codes[piece][:, cols].bitcast(FP8X4),
                    lhsT_scale=w_scales[piece][:, cols],
                    rhs=x_codes[g, dp][:].bitcast(FP8X4),
                    rhs_scale=x_scales[g, dp][:],
                    start=(dp == 0),
                    stop=(dp == D_PASSES - 1),
                )

        def y_tanh(n):
            s, g, i = units[n]
            tanh_y[n] = work.tile([P, PASS], F32, name="tanh_y", bufs=5, align_bytes=256)
            nc.scalar.activation(out=tanh_y[n][:], in_=y_bank[n][:], func=ACT.Tanh, bias=c_col(i), scale=1.0)

        def y_affine(n):
            s, g, i = units[n]
            if on_gpsimd(n):
                affine[n] = work.tile([P, PASS], F32, name="affine", bufs=3, align_bytes=256)
                nc.scalar.activation(out=affine[n][:], in_=tanh_y[n][:], func=ACT.Identity, bias=c_col(i), scale=k_col(i))

        def make_f_sum(n):
            s, g, i = units[n]
            f_sum[n] = work.tile([P, PASS], F32, name="f_sum", bufs=2, align_bytes=256)
            if on_gpsimd(n):
                nc.vector.tensor_tensor(out=f_sum[n][:], in0=affine[n][:], in1=y_bank[n][:], op=ALU.add)
            else:
                nc.vector.scalar_tensor_tensor(
                    out=f_sum[n][:], in0=tanh_y[n][:], scalar=k_col(i), in1=y_bank[n][:], op0=ALU.mult, op1=ALU.add
                )

        def make_f(n):
            s, g, i = units[n]
            a_row = a_rows[:, PASS * g : PASS * (g + 1)]
            fh_rounded[n, F] = work.tile([P, PASS], BF16, name="f_rounded", bufs=3, align_bytes=256)
            if on_gpsimd(n):
                nc.gpsimd.tensor_tensor(out=fh_rounded[n, F][:], in0=f_sum[n][:], in1=a_row, op=ALU.mult)
            else:
                nc.vector.scalar_tensor_tensor(
                    out=fh_rounded[n, F][:], in0=f_sum[n][:], scalar=c_col(i), in1=a_row, op0=ALU.add, op1=ALU.mult
                )

        def make_h(n):
            s, g, i = units[n]
            b_row = b_rows[:, PASS * g : PASS * (g + 1)]
            fh_rounded[n, H] = work.tile([P, PASS], BF16, name="h_rounded", bufs=3, align_bytes=256)
            nc.vector.scalar_tensor_tensor(
                out=fh_rounded[n, H][:], in0=y_bank[n][:], scalar=c_col(i), in1=b_row, op0=ALU.add, op1=ALU.mult
            )

        def elementwise(n):
            make_f_sum(n)
            if on_gpsimd(n):
                make_f(n)
                make_h(n)
            else:
                make_h(n)
                make_f(n)

        def turn(items):
            turned_fh = bank(rotate(turn_banks))
            for half, item in enumerate(items):
                words = fh_rounded[item][:].bitcast(F32)
                turned[item] = (turned_fh, half)
                for u in range(2):
                    at = P * (2 * half + u)
                    nc.tensor.transpose(turned_fh[:, at : at + P], words[:, u * P : (u + 1) * P], ident[:])

        def regroup(n, which):
            s, g, i = units[n]
            n_chunks = len(STEPS[s])
            if (s, g) not in fh_grouped:
                fh_grouped[s, g] = work.tile([P, 2 * n_chunks * PASS], BF16, name="fh_grouped", bufs=3, align_bytes=256)
            words = fh_grouped[s, g][:].bitcast(F32).rearrange("p (j i m u) -> p j i m u", j=2, i=n_chunks, u=2)
            turned_fh, half = turned[n, which[0]]
            src = turned_fh[:].rearrange("p (j u m) -> p j m u", j=2, u=2)
            nc.scalar.copy(out=words[:, which[0] : which[-1] + 1, STEPS[s].index(i), :, :], in_=src[:, half : half + len(which), :, :])

        def fh_quantise(n, which):
            s, g, i = units[n]
            if i != STEPS[s][-1]:
                return
            values = len(STEPS[s]) * PASS
            cols = slice(P * STEPS[s][0], P * (i + 1))
            for side in which:
                nc.vector.quantize_mx(
                    out=(h_codes, f_codes)[side][g][:, cols].bitcast(FP8X4),
                    scales=(h_scales, f_scales)[side][g][:, cols],
                    in_=fh_grouped[s, g][:, side * values : (side + 1) * values],
                )
                groups_quantised[s][side] = g + 1

        jobs = [job for step_jobs in JOBS for job in step_jobs]
        job_step = [s for s, step_jobs in enumerate(JOBS) for job in step_jobs]
        job_bank = []
        job_index = []
        passes_done = [0] * len(jobs)
        results = []
        stored = []

        def sums_of(j):
            sums = []
            place = 0
            for row0, rows, col0, width in jobs[j]:
                for row in range(row0, row0 + rows):
                    sums.append((row, col0, width, place))
                    place = place + width
            return sums

        def diagonal_places(j):
            return [place + P * row - col0 for row, col0, width, place in sums_of(j) if col0 <= P * row < col0 + width]

        def groups_ready(j):
            s = job_step[j]
            needs_f = any(row in STEPS[s] for row, col0, width, place in sums_of(j))
            return min(groups_quantised[s]) if needs_f else groups_quantised[s][H]

        def job_passes(limit=len(jobs)):
            while len(job_bank) < limit and free_job_banks and groups_ready(len(job_bank)) > 0:
                index = free_job_banks[0]
                free_job_banks.remove(index)
                job_bank.append(bank(index))
                job_index.append(index)
            for j in range(len(results), min(limit, len(job_bank))):
                sums = sums_of(j)
                for g in range(passes_done[j], groups_ready(j)):
                    for at, (row, col0, width, place) in enumerate(sums):
                        f_cols = slice(P * row, P * (row + 1))
                        h_cols = slice(col0, col0 + width)
                        nc.tensor.matmul_mx(
                            out=job_bank[j][:, place : place + width],
                            lhsT=f_codes[g][:, f_cols].bitcast(FP8X4),
                            lhsT_scale=f_scales[g][:, f_cols],
                            rhs=h_codes[g][:, h_cols].bitcast(FP8X4),
                            rhs_scale=h_scales[g][:, h_cols],
                            start=(g == 0 and at == 0),
                            stop=(g == GROUPS - 1 and at == len(sums) - 1),
                        )
                passes_done[j] = groups_ready(j)

        def result_tile():
            return work.tile([P, PASS], F32, name="result", bufs=6, align_bytes=256)

        def copy_out_scalar(j):
            result = result_tile()
            used = sum(width for row, col0, width, place in sums_of(j))
            nc.scalar.activation(out=result[:, 0:used], in_=job_bank[j][:, 0:used], func=ACT.Copy, scale=-1.0 / ROOT_N)
            return result

        def copy_out_vector(j):
            result = result_tile()
            (at,) = diagonal_places(j)
            plain = slice(P, PASS) if at == 0 else slice(0, at)
            block = slice(at, at + P)
            nc.vector.tensor_scalar(out=result[:, plain], in0=job_bank[j][:, plain], scalar1=-1.0 / ROOT_N, scalar2=None, op0=ALU.mult)
            nc.vector.scalar_tensor_tensor(
                out=result[:, block], in0=job_bank[j][:, block], scalar=-1.0 / ROOT_N, in1=root_ident[:], op0=ALU.mult, op1=ALU.add
            )
            return result

        def store(j, result):
            place = 0
            for row0, rows, col0, width in jobs[j]:
                nc.sync.dma_start(
                    out=out[P * row0 : P * (row0 + rows), col0 : col0 + width].rearrange("(r p) m -> p r m", p=P),
                    in_=result[:, place : place + rows * width].rearrange("p (r m) -> p r m", r=rows),
                )
                place = place + rows * width

        def finish_next():
            j = len(results)
            if passes_done[j] == GROUPS:
                results.append(copy_out_scalar(j))
                free_job_banks.append(job_index[j])

        def store_up_to(count):
            for j in range(len(stored), count):
                for at in diagonal_places(j):
                    block = results[j][:, at : at + P]
                    nc.vector.tensor_tensor(out=block, in0=block, in1=root_ident[:], op=ALU.add)
                store(j, results[j])
                stored.append(j)

        for piece in range(W_ON_GPSIMD - 1):
            w_interleave_gpsimd(piece, w_tile(piece))
        for part in range(X_ALONE):
            x_widen(part)
            if part >= 6:
                y_affine(part - 6)
            if part in (4, 5):
                w_interleave_scalar(W_ON_GPSIMD, part - 4)
            x_turn(part)
            if part == 1:
                make_ck()
            if part < 2:
                spread_ab(part, 0, unit_banks[part])
            if part in (AB_SECOND_HALF, AB_SECOND_HALF + 1):
                spread_ab(part - AB_SECOND_HALF, 1, SETUP_BANK)
            if part == 4:
                for piece in range(W_ON_GPSIMD - 1):
                    w_quantise(piece)
                x_quantise(0)
            if part == 5:
                x_quantise(1)
                w_interleave_gpsimd(W_ON_GPSIMD - 1, x_grouped[0, 1][:, 0 : 4 * W_COLS])
            if part in (5, 6):
                y_matmul(part - 5)
                y_tanh(part - 5)
            if part == 7:
                w_quantise(W_ON_GPSIMD - 1)
                x_quantise(2)

        for n in range(MIXED):
            part = X_ALONE + n
            elementwise(n)
            y_matmul(n + 2)
            y_tanh(n + 2)
            if n < 2:
                w_interleave_scalar(W_ON_GPSIMD + 1, n)
            y_affine(n + 2)
            x_widen(part)
            if part % 2 == 1:
                x_quantise((part - 3) // 2)
            if n >= 2:
                fh_quantise(n - 2, BOTH)
            if n in (3, 5):
                w_quantise(W_ON_GPSIMD + (n - 3) // 2)
            turn([(n, H), (n, F)])
            regroup(n, BOTH)
            x_turn(part)
            job_passes()

        turn_banks.remove(THIRD_UNIT_BANK)
        unit_banks.clear()
        unit_banks.extend([THIRD_UNIT_BANK, y_index[MIXED], y_index[MIXED + 1]])
        free_job_banks.extend(SCALE_BANKS)
        y_matmul(MIXED + 2)
        y_tanh(MIXED + 2)
        y_affine(MIXED + 2)

        last_pieces = (2 * D_PASSES + 2, 2 * D_PASSES + 3)
        first_of_chunk_6 = last_chunk - GROUPS
        not_quantised = MIXED - 2
        for n in range(MIXED, last_chunk, 2):
            pair = (n, n + 1)
            copied_out = len(results)
            job_passes()
            for m in pair:
                elementwise(m)
                if (units[m + 3][1], D_PASSES - 1) in x_codes:
                    y_matmul(m + 3)
                    finish_next()
                    y_tanh(m + 3)
            for m in pair:
                turn([(m, H), (m, F)])
            store_up_to(copied_out)
            for m in range(not_quantised, n):
                fh_quantise(m, BOTH)
            not_quantised = n
            if n + 6 == first_of_chunk_6:
                for piece in last_pieces:
                    w_quantise(piece)
            if n == MIXED:
                x_quantise(GROUPS * D_PASSES - 1)
                y_matmul(n + 4)
            for m in pair:
                regroup(m, BOTH)
            if n == MIXED:
                y_tanh(n + 4)
            for m in pair:
                y_affine(m + 3)
            if n < MIXED + 8:
                dp, half = divmod((n - MIXED) // 2, 2)
                w_interleave_scalar(last_pieces[dp], half)

        n0, n1, n2, n3 = range(last_chunk, len(units))
        first_of_step = len(jobs) - len(JOBS[-1])
        first_of_row_7 = len(jobs) - 3
        job_passes()
        make_f_sum(n0)
        make_h(n0)
        y_matmul(n3)
        finish_next()
        y_tanh(n3)
        make_h(n1)
        make_f(n0)
        turn([(n0, H), (n0, F)])
        regroup(n0, BOTH)
        job_passes()
        for m in range(not_quantised, n0):
            fh_quantise(m, BOTH)
        job_passes(first_of_step - 1)
        finish_next()

        make_f_sum(n1)
        free_job_banks.append(y_index[n1])
        make_h(n2)
        store_up_to(len(results))
        turn([(n1, H), (n2, H)])
        regroup(n1, (H,))
        regroup(n2, (H,))
        job_passes(first_of_step)
        finish_next()
        make_f(n1)
        make_h(n3)
        fh_quantise(n0, BOTH)
        turn([(n1, F), (n3, H)])
        regroup(n3, (H,))
        regroup(n1, (F,))
        finish_next()
        store_up_to(len(results))
        job_passes(first_of_row_7)

        make_f_sum(n2)
        fh_quantise(n1, (H,))
        fh_quantise(n2, (H,))
        job_passes(first_of_step + 1)
        make_f(n2)
        turn([(n2, F)])
        regroup(n2, (F,))
        job_passes(first_of_row_7)
        free_job_banks.append(y_index[n2])

        make_f_sum(n3)
        fh_quantise(n3, (H,))
        fh_quantise(n1, (F,))
        job_passes(first_of_step + 1)
        make_f(n3)
        turn([(n3, F)])
        regroup(n3, (F,))
        finish_next()
        job_passes(first_of_row_7)
        fh_quantise(n2, (F,))
        job_passes(first_of_row_7 + 1)
        fh_quantise(n3, (F,))
        job_passes()
        store_up_to(len(results))
        for j in (first_of_row_7 - 1, first_of_row_7):
            store(j, copy_out_vector(j))
        for j in (first_of_row_7 + 1, first_of_row_7 + 2):
            store(j, copy_out_scalar(j))
